import numpy as np
import ml_dtypes


def mxq(x, axis, fmt="e4m3"):
    dtype, down = {"e4m3": (ml_dtypes.float8_e4m3fn, 7), "e5m2": (ml_dtypes.float8_e5m2, 14)}[fmt]
    v = np.moveaxis(np.asarray(x, np.float32).astype(ml_dtypes.bfloat16).astype(np.float64), axis, -1)
    blocks = v.reshape(v.shape[:-1] + (-1, 32))
    amax = np.abs(blocks).max(-1, keepdims=True)
    byte = np.maximum(np.where(amax > 0, np.frexp(amax)[1] - 1 + 127, 0) - down, 1)
    scale = np.exp2(byte - 127.0)
    codes = (blocks / scale).astype(np.float32).astype(dtype).astype(np.float64)
    return np.moveaxis((codes * scale).reshape(v.shape), -1, axis)


WIDE = False


def mx_kscale(k):
    if not WIDE:
        return np.ones(k)
    levels = np.array([24, -24, 12, -12, 0])
    if k % 512:
        return np.exp2(np.random.permutation(np.resize(levels, k // 32))).repeat(32)
    a = np.empty((k // 512, 16))
    for p in range(k // 512):
        a[p, :8] = np.random.permutation(np.resize(levels, 8))
        for g in range(8):
            far = levels[np.abs(levels - a[p, g]) >= 10]
            a[p, g + 8] = far[np.random.randint(len(far))]
    return np.exp2(a.ravel()).repeat(32)


def f64(x):
    return np.asarray(x).astype(np.float64)


def striped(idx):
    return np.tile(idx.reshape(-1, 16).T, (8, 1)).astype(np.uint16)


def unstriped(offs):
    return offs[:16].T.reshape(-1).astype(np.int64)


E2M1 = np.array([0.0, 0.5, 1.0, 1.5, 2.0, 3.0, 4.0, 6.0, -0.0, -0.5, -1.0, -1.5, -2.0, -3.0, -4.0, -6.0])


def pack_weight(w, fmt):
    k, n = w.shape
    w = f64(np.asarray(w, np.float32).astype(ml_dtypes.bfloat16)).reshape(k // 32, 32, n)
    amax = np.abs(w).max(1)
    if fmt == "e4m3":
        byte = np.frexp(amax)[1] - 1 + 127 - 7
    else:
        mant, ex = np.frexp(amax / 6.0)
        byte = np.where(mant > 0.5, ex, ex - 1) + 127
    byte = np.clip(np.where(amax > 0, byte, 1), 1, 254)
    scaled = (w * np.exp2(127.0 - byte)[:, None, :]).reshape(k, n).astype(np.float32)
    by_word = np.ascontiguousarray(scaled.reshape(k // 512, 128, 4, n).transpose(0, 1, 3, 2))
    if fmt == "e4m3":
        words = by_word.astype(ml_dtypes.float8_e4m3fn).view(np.uint8)
    else:
        c = by_word.astype(ml_dtypes.float4_e2m1fn).view(np.uint8) & 0xF
        words = (c[..., 0::2] | (c[..., 1::2] << 4)).reshape(k // 512, 128, 2 * n)
    return np.ascontiguousarray(words), np.ascontiguousarray(byte.astype(np.uint8).reshape(k // 512, 16, n))


def unpack_weight(words, scales, fmt):
    g, _, n = scales.shape
    words = np.ascontiguousarray(words).reshape(g, 128, n, -1)
    if fmt == "e4m3":
        vals = words.view(ml_dtypes.float8_e4m3fn).astype(np.float64)
    else:
        nib = np.empty((g, 128, n, 4), np.uint8)
        nib[..., 0::2] = words & 0xF
        nib[..., 1::2] = words >> 4
        vals = E2M1[nib]
    vals = vals * np.repeat(np.exp2(scales.astype(np.float64) - 127.0), 8, axis=1)[..., None]
    return vals.transpose(0, 1, 3, 2).reshape(g * 512, n)


def pack_table4(v):
    words, scales = pack_weight(v, "e2m1")
    g, t = words.shape[0] // 2, v.shape[1]
    return np.ascontiguousarray(words.reshape(g, 2, 128, t, 2).transpose(0, 2, 3, 1, 4).reshape(g, 128, t, 4)), scales


def unpack_table4(words, scales):
    g, _, t, _ = words.shape
    return unpack_weight(words.reshape(g, 128, t, 2, 2).transpose(0, 3, 1, 2, 4).reshape(2 * g, 128, 2 * t), scales, "e2m1")


K, R, N, T, J = 1024, 512, 512, 2048, 1024


def setup_inputs():
    n = np.random.standard_normal
    s = mx_kscale(K)[:, None]
    u = mx_kscale(R)[:, None]
    wd = n((R, N)) / np.sqrt(R) / u
    wd4 = pack_weight(wd, "e2m1")
    wdrest = wd - unpack_weight(*wd4, "e2m1")
    p_tab = pack_table4(n((K, T)) * s)
    p_wu = pack_weight(n((K, R)) / np.sqrt(K) / s * u.T, "e2m1")
    p_wd8 = pack_weight(wdrest, "e4m3")
    return {
        "tab_words": p_tab[0],
        "tab_scales": p_tab[1],
        "wg": (n((K, R)) / np.sqrt(K) / s).astype(np.float32),
        "wu_words": p_wu[0],
        "wu_scales": p_wu[1],
        "wd4_words": wd4[0],
        "wd4_scales": wd4[1],
        "wd8_words": p_wd8[0],
        "wd8_scales": p_wd8[1],
        "offs": striped(np.random.permutation(T)[:J]),
    }


def reference(tab_words, tab_scales, wg, wu_words, wu_scales, wd4_words, wd4_scales, wd8_words, wd8_scales, offs):
    idx = unstriped(offs)
    tab_ = unpack_table4(tab_words, tab_scales)[:, idx]
    wg_ = mxq(f64(wg), 0, "e4m3")
    wu_ = unpack_weight(wu_words, wu_scales, "e2m1")
    ga = wg_.T @ tab_
    ub = wu_.T @ tab_
    h = np.tanh(ga) * ub
    h_ = mxq(h, 0, "e4m3")
    wd4_ = unpack_weight(wd4_words, wd4_scales, "e2m1")
    wd8_ = unpack_weight(wd8_words, wd8_scales, "e4m3")
    y = wd4_.T @ h_ + wd8_.T @ h_
    return y

@@ -1,0 +1,212 @@
+from contextlib import ExitStack
+
+import concourse.mybir as mybir
+
+K, R, N, T, J = 1024, 512, 512, 2048, 1024
+FLOPS = 2 * (2 * K * R * J + 2 * R * N * J)
+
+F32 = mybir.dt.float32
+BF16 = mybir.dt.bfloat16
+I32 = mybir.dt.int32
+U32 = mybir.dt.uint32
+U16 = mybir.dt.uint16
+U8 = mybir.dt.uint8
+FP8X4 = mybir.dt.float8_e4m3fn_x4
+FP4X4 = mybir.dt.float4_e2m1fn_x4
+TANH = mybir.ActivationFunctionType.Tanh
+MULT = mybir.AluOpType.mult
+
+P = 128
+PACK = 4
+K_PASS = P * PACK
+PASSES = K // K_PASS
+CHUNK = 128
+CHUNKS = J // CHUNK
+PIECE = 256
+PIECES = J // PIECE
+UP_BANKS = 6
+HALF = R // 2
+
+
+def tile_list_gmlpt_tanh_res_none_kernel(
+    tc, tab_words, tab_scales, wg, wu_words, wu_scales, wd4_words, wd4_scales, wd8_words, wd8_scales, offs, out
+):
+    nc = tc.nc
+    with ExitStack() as ctx:
+        keep = ctx.enter_context(tc.tile_pool(name="keep", bufs=1))
+        ring = ctx.enter_context(tc.tile_pool(name="ring", bufs=4))
+        psum = ctx.enter_context(tc.psum_pool(name="psum", bufs=1))
+
+        offsets = keep.tile([P, J // 16], U16, name="offsets")
+        tab_w = keep.tile([P, T], I32, name="tab_w", align_bytes=64)
+        tab_s = keep.tile([P, PASSES, T // 4], I32, name="tab_s", align_bytes=64)
+        wu_w_raw = keep.tile([P, PASSES, R // 2], I32, name="wu_w_raw", align_bytes=64)
+        wu_s_raw = keep.tile([P, PASSES, R // 4], I32, name="wu_s_raw", align_bytes=64)
+        wu_w = keep.tile([P, PASSES, 2 * R], U8, name="wu_w", align_bytes=64)
+        wu_s = keep.tile([P, PASSES, R], U8, name="wu_s", align_bytes=64)
+        wd4_w = keep.tile([P, N // 2], I32, name="wd4_w", align_bytes=64)
+        wd8_w = keep.tile([P, N], I32, name="wd8_w", align_bytes=64)
+        wd_s = keep.tile([P, 2, N // 4], I32, name="wd_s", align_bytes=64)
+        wg_raw = keep.tile([P, PASSES, 2, PACK, HALF], F32, name="wg_raw", align_bytes=64)
+        wg_bf = keep.tile([P, PASSES, PACK, P, PACK], BF16, name="wg_bf", align_bytes=64)
+        wg_w = keep.tile([P, PASSES, R], U32, name="wg_w", align_bytes=64)
+        wg_s = keep.tile([P, PASSES, R], U8, name="wg_s", align_bytes=64)
+        got_w = keep.tile([P, J], U32, name="got_w", align_bytes=64)
+        got_s = keep.tile([P, PASSES, J], U8, name="got_s", align_bytes=64)
+        v_w = keep.tile([P, PASSES, 2 * J], U8, name="v_w", align_bytes=64)
+        h_w = keep.tile([P, J], U32, name="h_w", align_bytes=64)
+        h_s = keep.tile([P, J], U8, name="h_s", align_bytes=64)
+        warm = keep.tile([P, 8], F32, name="warm")
+        warm_out = keep.tile([P, 8], F32, name="warm_out")
+        banks = [psum.tile([P, PACK, CHUNK], F32, name="bank%d" % b) for b in range(8)]
+
+        nc.vector.memset(wu_s_raw[:], 0)
+        nc.vector.memset(tab_s[:], 0)
+        nc.vector.memset(warm[:], 0.0)
+        nc.vector.memset(wd_s[:], 0)
+        nc.scalar.activation(warm_out[:], warm[:], TANH)
+
+        def load_scales(queue, tile_rows, scales):
+            rows = scales.bitcast(I32)
+            for r in range(4):
+                queue.dma_start(out=tile_rows(r), in_=rows[:, r:16:4, :].rearrange("a q w -> q a w"))
+
+        nc.sync.dma_start(offsets[:], offs)
+        load_scales(nc.sync, lambda r: wu_s_raw[r:P:32, :, :], wu_scales)
+        nc.sync.dma_start(out=wu_w_raw[:], in_=wu_words.bitcast(I32).rearrange("a p w -> p a w"))
+        nc.sync.dma_start(out=tab_w[:], in_=tab_words[0].rearrange("p t b -> p (t b)").bitcast(I32))
+        load_scales(nc.sync, lambda r: tab_s[r:P:32, :, :], tab_scales)
+        for a in range(PASSES):
+            for u in range(2):
+                rows = wg[a * K_PASS : (a + 1) * K_PASS, u * HALF : (u + 1) * HALF]
+                nc.sync.dma_start(out=wg_raw[:, a, u, :, :], in_=rows.rearrange("(p i) r -> p i r", i=PACK))
+        nc.sync.dma_start(out=wd4_w[:], in_=wd4_words[0].bitcast(I32))
+        nc.sync.dma_start(out=wd8_w[:], in_=wd8_words[0].rearrange("p n b -> p (n b)").bitcast(I32))
+        load_scales(nc.sync, lambda r: wd_s[r:P:32, 0:1, :], wd4_scales)
+        load_scales(nc.sync, lambda r: wd_s[r:P:32, 1:2, :], wd8_scales)
+
+        nc.vector.tensor_copy(
+            out=wu_w[:].bitcast(U16).rearrange("p a (t m) -> p a t m", t=PACK),
+            in_=wu_w_raw[:].bitcast(U16).rearrange("p a (m t) -> p a t m", t=PACK),
+        )
+        nc.vector.tensor_copy(
+            out=wu_s[:].rearrange("p a (t m) -> p a t m", t=PACK),
+            in_=wu_s_raw[:].bitcast(U8).rearrange("p a (m t) -> p a t m", t=PACK),
+        )
+
+        def listed(g):
+            return offsets[:, g * (PIECE // 16) : (g + 1) * (PIECE // 16)]
+
+        def gather_words(g):
+            cols = slice(g * PIECE, (g + 1) * PIECE)
+            nc.vector.tensor_copy(out=got_w[:, cols], in_=tab_w[:].bitcast(U32).indirect(listed(g)))
+
+        def part_words(g):
+            cols = slice(g * PIECE, (g + 1) * PIECE)
+            nc.vector.tensor_copy(
+                out=v_w[:].bitcast(U16)[:, :, cols],
+                in_=got_w[:, cols].bitcast(U16).rearrange("p (j a) -> p a j", a=PASSES),
+            )
+
+        def gather_scales(g):
+            cols = slice(g * PIECE, (g + 1) * PIECE)
+            for a in range(PASSES):
+                nc.vector.tensor_copy(out=got_s[:, a, cols], in_=tab_s[:, a, :].bitcast(U8).indirect(listed(g)))
+
+        def cast_wg(a, u):
+            half = slice(u * (P // 2), (u + 1) * (P // 2))
+            nc.scalar.copy(
+                out=wg_bf[:, a, :, half, :].rearrange("p t m i -> p m i t"),
+                in_=wg_raw[:, a, u, :, :].rearrange("p i (m t) -> p m i t", t=PACK),
+            )
+
+        def quantize_wg(a, t0, t1):
+            cols = slice(t0 * P, t1 * P)
+            nc.vector.quantize_mx(
+                out=wg_w[:, a, cols].bitcast(FP8X4),
+                scales=wg_s[:, a, cols],
+                in_=wg_bf[:, a, t0:t1, :, :].rearrange("p t m i -> p (t m i)"),
+            )
+
+        def up_bank(c):
+            return banks[c % UP_BANKS]
+
+        def gate_bank(c):
+            return banks[UP_BANKS + c % 2]
+
+        def first_layer(bank, c, weight, weight_scale):
+            for t in range(PACK):
+                for a in range(PASSES):
+                    nc.tensor.matmul_mx(
+                        out=bank[:, t, :],
+                        lhsT=weight(a, t),
+                        lhsT_scale=weight_scale[:, a, t * P : (t + 1) * P],
+                        rhs=v_w[:, a, 2 * c * CHUNK : 2 * (c + 1) * CHUNK].bitcast(FP4X4),
+                        rhs_scale=got_s[:, a, c * CHUNK : (c + 1) * CHUNK],
+                        start=(a == 0),
+                        stop=(a == PASSES - 1),
+                    )
+
+        def up(c):
+            first_layer(up_bank(c), c, lambda a, t: wu_w[:, a, 2 * t * P : 2 * (t + 1) * P].bitcast(FP4X4), wu_s)
+
+        def gate(c):
+            first_layer(gate_bank(c), c, lambda a, t: wg_w[:, a, t * P : (t + 1) * P].bitcast(FP8X4), wg_s)
+
+        def hidden(c):
+            cols = slice(c * CHUNK, (c + 1) * CHUNK)
+            gated = ring.tile([P, CHUNK, PACK], F32, name="gated")
+            nc.scalar.activation(gated[:], gate_bank(c)[:].rearrange("p t j -> p j t"), TANH)
+            h_bf = ring.tile([P, CHUNK, PACK], BF16, name="h_bf", align_bytes=64)
+            nc.vector.tensor_tensor(h_bf[:], up_bank(c)[:].rearrange("p t j -> p j t"), gated[:], MULT)
+            nc.vector.quantize_mx(
+                out=h_w[:, cols].bitcast(FP8X4), scales=h_s[:, cols], in_=h_bf[:].rearrange("p j t -> p (j t)")
+            )
+
+        def down(c):
+            cols = slice(c * CHUNK, (c + 1) * CHUNK)
+            bank = up_bank(c)
+            for b in range(N // P):
+                tiers = (
+                    wd4_w[:].bitcast(U8)[:, 2 * b * P : 2 * (b + 1) * P].bitcast(FP4X4),
+                    wd8_w[:, b * P : (b + 1) * P].bitcast(FP8X4),
+                )
+                for tier in range(2):
+                    nc.tensor.matmul_mx(
+                        out=bank[:, b, :],
+                        lhsT=tiers[tier],
+                        lhsT_scale=wd_s[:, tier, :].bitcast(U8)[:, b * P : (b + 1) * P],
+                        rhs=h_w[:, cols].bitcast(FP8X4),
+                        rhs_scale=h_s[:, cols],
+                        start=(tier == 0),
+                        stop=(tier == 1),
+                    )
+            staged = ring.tile([P, N // P, CHUNK], F32, name="staged")
+            nc.scalar.copy(out=staged[:], in_=bank[:])
+            nc.sync.dma_start(out=out[:, cols].rearrange("(b p) j -> p b j", p=P), in_=staged[:])
+
+        for a in range(PASSES):
+            for u in range(2):
+                cast_wg(a, u)
+        quantize_wg(0, 0, PACK)
+        quantize_wg(1, 0, 2)
+        quantize_wg(1, 2, PACK)
+
+        for g in range(3):
+            gather_words(g)
+            gather_scales(g)
+            part_words(g)
+        for c in range(UP_BANKS):
+            up(c)
+        for c in range(CHUNKS):
+            gate(c)
+            if c == 2:
+                gather_words(3)
+                gather_scales(3)
+                part_words(3)
+            if c >= UP_BANKS:
+                up(c)
+            hidden(c)
+            if c >= 1:
+                down(c - 1)
+        down(CHUNKS - 1)

@@ -15,6 +15,7 @@ FP8X4 = mybir.dt.float8_e4m3fn_x4
 FP4X4 = mybir.dt.float4_e2m1fn_x4
 TANH = mybir.ActivationFunctionType.Tanh
 MULT = mybir.AluOpType.mult
+ADD = mybir.AluOpType.add
 
 P = 128
 PACK = 4
@@ -22,10 +23,15 @@ K_PASS = P * PACK
 PASSES = K // K_PASS
 CHUNK = 128
 CHUNKS = J // CHUNK
-PIECE = 256
-PIECES = J // PIECE
-UP_BANKS = 6
-HALF = R // 2
+PIECES = [(0, 256), (256, 512), (512, 768), (768, 1024)]
+WG_PARTS = [(0, 0, 64), (0, 64, 128), (1, 0, 64), (1, 64, 128)]
+CASTS = [(0, 0, 64, 'a'), (1, 64, 128, 'a'), (2, 0, 64, 'a'), (3, 64, 96, 'a'), (3, 96, 128, 'v')]
+STORES = [(0, 1), (1, 1), (2, 1), (3, 1), (4, 1), (5, 1), (6, 1), (7, 1)]
+UP_BANK = [0, 1, 2, 3, 4, 0, 1, 2]
+GATE_BANK = [5, 6, 7, 5, 6, 7, 5, 6]
+HELD = 4
+LOADS = [(('zero', 'wu'), 'v'), (('zero', 'tab'), 'v'), (('zero', 'wd'), 'v'), (('zero', 'warm'), 'v'), (('offs', 0), 's'), (('wuw', 0), 's'), (('tabs', 0), 's'), (('tabs', 1), 's'), (('tabs', 2), 's'), (('tabs', 3), 's'), (('wus', 0), 'a'), (('wus', 1), 'a'), (('wus', 2), 'a'), (('wus', 3), 'a'), (('tabw', 0), 's'), (('warm', 0), 'a'), (('wg', 0), 's'), (('wg', 1), 's'), (('wg', 2), 's'), (('wg', 3), 's'), (('wd4w', 0), 's'), (('wd8w', 0), 's'), (('wd4s', 0), 's'), (('wd4s', 1), 's'), (('wd4s', 2), 's'), (('wd4s', 3), 's'), (('wd8s', 0), 's'), (('wd8s', 1), 's'), (('wd8s', 2), 's'), (('wd8s', 3), 's')]
+ORDER = [('pw', 0), ('ps', 0), ('W', 0), ('P', 0), ('S', 0, 0), ('S', 0, 1), ('u', 0), ('u', 1), ('W', 1), ('P', 1), ('S', 1, 0), ('S', 1, 1), ('u', 2), ('u', 3), ('W', 2), ('P', 2), ('S', 2, 0), ('S', 2, 1), ('u', 4), ('cast', 0), ('cast', 1), ('cast', 2), ('cast', 3), ('cast', 4), ('q', 0, 0, 4), ('q', 1, 0, 1), ('q', 1, 1, 2), ('q', 1, 2, 4), ('g', 0), ('t', 0), ('m', 0), ('W', 3), ('P', 3), ('S', 3, 0), ('S', 3, 1), ('g', 1), ('t', 1), ('m', 1), ('n', 0), ('g', 2), ('t', 2), ('m', 2), ('n', 1), ('g', 3), ('t', 3), ('m', 3), ('n', 2), ('g', 4), ('t', 4), ('m', 4), ('n', 3), ('g', 5), ('u', 5), ('t', 5), ('m', 5), ('n', 4), ('g', 6), ('u', 6), ('t', 6), ('m', 6), ('n', 5), ('g', 7), ('u', 7), ('t', 7), ('m', 7), ('n', 6), ('D', 0, 3, 0, 'a'), ('D', 1, 4, 0, 'a'), ('D', 2, 7, 0, 'a'), ('D', 3, 0, 0, 'a'), ('n', 7), ('D', 0, 5, 1, 'a'), ('D', 1, 1, 1, 'v'), ('D', 2, 6, 1, 'a'), ('D', 3, 2, 1, 'v')]
 
 
 def tile_list_gmlpt_tanh_res_none_kernel(
@@ -35,6 +41,7 @@ def tile_list_gmlpt_tanh_res_none_kernel(
     with ExitStack() as ctx:
         keep = ctx.enter_context(tc.tile_pool(name="keep", bufs=1))
         ring = ctx.enter_context(tc.tile_pool(name="ring", bufs=4))
+        held = ctx.enter_context(tc.tile_pool(name="held", bufs=HELD))
         psum = ctx.enter_context(tc.psum_pool(name="psum", bufs=1))
 
         offsets = keep.tile([P, J // 16], U16, name="offsets")
@@ -47,166 +54,179 @@ def tile_list_gmlpt_tanh_res_none_kernel(
         wd4_w = keep.tile([P, N // 2], I32, name="wd4_w", align_bytes=64)
         wd8_w = keep.tile([P, N], I32, name="wd8_w", align_bytes=64)
         wd_s = keep.tile([P, 2, N // 4], I32, name="wd_s", align_bytes=64)
-        wg_raw = keep.tile([P, PASSES, 2, PACK, HALF], F32, name="wg_raw", align_bytes=64)
+        wg_raw = [keep.tile([P, PACK, PACK * (m1 - m0)], F32, name="wg_raw%d" % i, align_bytes=64) for i, (a, m0, m1) in enumerate(WG_PARTS)]
         wg_bf = keep.tile([P, PASSES, PACK, P, PACK], BF16, name="wg_bf", align_bytes=64)
         wg_w = keep.tile([P, PASSES, R], U32, name="wg_w", align_bytes=64)
         wg_s = keep.tile([P, PASSES, R], U8, name="wg_s", align_bytes=64)
-        got_w = keep.tile([P, J], U32, name="got_w", align_bytes=64)
-        got_s = keep.tile([P, PASSES, J], U8, name="got_s", align_bytes=64)
-        v_w = keep.tile([P, PASSES, 2 * J], U8, name="v_w", align_bytes=64)
+        got, v_w, v_s = {}, {}, {}
         h_w = keep.tile([P, J], U32, name="h_w", align_bytes=64)
         h_s = keep.tile([P, J], U8, name="h_s", align_bytes=64)
         warm = keep.tile([P, 8], F32, name="warm")
         warm_out = keep.tile([P, 8], F32, name="warm_out")
         banks = [psum.tile([P, PACK, CHUNK], F32, name="bank%d" % b) for b in range(8)]
+        staged, gated, h_bf = {}, {}, {}
+        queues = {"s": nc.sync, "a": nc.scalar, "g": nc.gpsimd}
 
-        nc.vector.memset(wu_s_raw[:], 0)
-        nc.vector.memset(tab_s[:], 0)
-        nc.vector.memset(warm[:], 0.0)
-        nc.vector.memset(wd_s[:], 0)
-        nc.scalar.activation(warm_out[:], warm[:], TANH)
+        def scale_rows(queue, tile_rows, scales, r):
+            queue.dma_start(out=tile_rows, in_=scales.bitcast(I32)[:, r:16:4, :].rearrange("a q w -> q a w"))
 
-        def load_scales(queue, tile_rows, scales):
-            rows = scales.bitcast(I32)
-            for r in range(4):
-                queue.dma_start(out=tile_rows(r), in_=rows[:, r:16:4, :].rearrange("a q w -> q a w"))
-
-        nc.sync.dma_start(offsets[:], offs)
-        load_scales(nc.sync, lambda r: wu_s_raw[r:P:32, :, :], wu_scales)
-        nc.sync.dma_start(out=wu_w_raw[:], in_=wu_words.bitcast(I32).rearrange("a p w -> p a w"))
-        nc.sync.dma_start(out=tab_w[:], in_=tab_words[0].rearrange("p t b -> p (t b)").bitcast(I32))
-        load_scales(nc.sync, lambda r: tab_s[r:P:32, :, :], tab_scales)
-        for a in range(PASSES):
-            for u in range(2):
-                rows = wg[a * K_PASS : (a + 1) * K_PASS, u * HALF : (u + 1) * HALF]
-                nc.sync.dma_start(out=wg_raw[:, a, u, :, :], in_=rows.rearrange("(p i) r -> p i r", i=PACK))
-        nc.sync.dma_start(out=wd4_w[:], in_=wd4_words[0].bitcast(I32))
-        nc.sync.dma_start(out=wd8_w[:], in_=wd8_words[0].rearrange("p n b -> p (n b)").bitcast(I32))
-        load_scales(nc.sync, lambda r: wd_s[r:P:32, 0:1, :], wd4_scales)
-        load_scales(nc.sync, lambda r: wd_s[r:P:32, 1:2, :], wd8_scales)
-
-        nc.vector.tensor_copy(
-            out=wu_w[:].bitcast(U16).rearrange("p a (t m) -> p a t m", t=PACK),
-            in_=wu_w_raw[:].bitcast(U16).rearrange("p a (m t) -> p a t m", t=PACK),
-        )
-        nc.vector.tensor_copy(
-            out=wu_s[:].rearrange("p a (t m) -> p a t m", t=PACK),
-            in_=wu_s_raw[:].bitcast(U8).rearrange("p a (m t) -> p a t m", t=PACK),
-        )
+        def load(what, q):
+            queue = queues.get(q)
+            kind, i = what
+            if kind == "offs":
+                nc.sync.dma_start(offsets[:], offs)
+            elif kind == "wuw":
+                queue.dma_start(out=wu_w_raw[:], in_=wu_words.bitcast(I32).rearrange("a p w -> p a w"))
+            elif kind == "tabw":
+                queue.dma_start(out=tab_w[:], in_=tab_words[0].rearrange("p t b -> p (t b)").bitcast(I32))
+            elif kind == "wus":
+                scale_rows(queue, wu_s_raw[i:P:32, :, :], wu_scales, i)
+            elif kind == "tabs":
+                scale_rows(queue, tab_s[i:P:32, :, :], tab_scales, i)
+            elif kind == "wd4s":
+                scale_rows(queue, wd_s[i:P:32, 0:1, :], wd4_scales, i)
+            elif kind == "wd8s":
+                scale_rows(queue, wd_s[i:P:32, 1:2, :], wd8_scales, i)
+            elif kind == "wg":
+                a, m0, m1 = WG_PARTS[i]
+                rows = wg[a * K_PASS : (a + 1) * K_PASS, PACK * m0 : PACK * m1]
+                queue.dma_start(out=wg_raw[i][:], in_=rows.rearrange("(p i) r -> p i r", i=PACK))
+            elif kind == "wd4w":
+                queue.dma_start(out=wd4_w[:], in_=wd4_words[0].bitcast(I32))
+            elif kind == "wd8w":
+                queue.dma_start(out=wd8_w[:], in_=wd8_words[0].rearrange("p n b -> p (n b)").bitcast(I32))
+            elif kind == "warm":
+                nc.scalar.activation(warm_out[:], warm[:], TANH)
+            elif kind == "zero":
+                (nc.vector if q == "v" else nc.gpsimd).memset({"tab": tab_s, "wu": wu_s_raw, "wd": wd_s, "warm": warm}[i][:], 0)
 
         def listed(g):
-            return offsets[:, g * (PIECE // 16) : (g + 1) * (PIECE // 16)]
-
-        def gather_words(g):
-            cols = slice(g * PIECE, (g + 1) * PIECE)
-            nc.vector.tensor_copy(out=got_w[:, cols], in_=tab_w[:].bitcast(U32).indirect(listed(g)))
-
-        def part_words(g):
-            cols = slice(g * PIECE, (g + 1) * PIECE)
-            nc.vector.tensor_copy(
-                out=v_w[:].bitcast(U16)[:, :, cols],
-                in_=got_w[:, cols].bitcast(U16).rearrange("p (j a) -> p a j", a=PASSES),
-            )
-
-        def gather_scales(g):
-            cols = slice(g * PIECE, (g + 1) * PIECE)
-            for a in range(PASSES):
-                nc.vector.tensor_copy(out=got_s[:, a, cols], in_=tab_s[:, a, :].bitcast(U8).indirect(listed(g)))
-
-        def cast_wg(a, u):
-            half = slice(u * (P // 2), (u + 1) * (P // 2))
-            nc.scalar.copy(
-                out=wg_bf[:, a, :, half, :].rearrange("p t m i -> p m i t"),
-                in_=wg_raw[:, a, u, :, :].rearrange("p i (m t) -> p m i t", t=PACK),
-            )
-
-        def quantize_wg(a, t0, t1):
-            cols = slice(t0 * P, t1 * P)
-            nc.vector.quantize_mx(
-                out=wg_w[:, a, cols].bitcast(FP8X4),
-                scales=wg_s[:, a, cols],
-                in_=wg_bf[:, a, t0:t1, :, :].rearrange("p t m i -> p (t m i)"),
-            )
-
-        def up_bank(c):
-            return banks[c % UP_BANKS]
-
-        def gate_bank(c):
-            return banks[UP_BANKS + c % 2]
+            return offsets[:, PIECES[g][0] // 16 : PIECES[g][1] // 16]
 
         def first_layer(bank, c, weight, weight_scale):
+            g = [i for i, (j0, j1) in enumerate(PIECES) if j0 <= c * CHUNK < j1][0]
+            lo = c * CHUNK - PIECES[g][0]
             for t in range(PACK):
                 for a in range(PASSES):
                     nc.tensor.matmul_mx(
                         out=bank[:, t, :],
                         lhsT=weight(a, t),
                         lhsT_scale=weight_scale[:, a, t * P : (t + 1) * P],
-                        rhs=v_w[:, a, 2 * c * CHUNK : 2 * (c + 1) * CHUNK].bitcast(FP4X4),
-                        rhs_scale=got_s[:, a, c * CHUNK : (c + 1) * CHUNK],
+                        rhs=v_w[g][:, a, 2 * lo : 2 * (lo + CHUNK)].bitcast(FP4X4),
+                        rhs_scale=v_s[g][:, a, lo : lo + CHUNK],
                         start=(a == 0),
                         stop=(a == PASSES - 1),
                     )
 
-        def up(c):
-            first_layer(up_bank(c), c, lambda a, t: wu_w[:, a, 2 * t * P : 2 * (t + 1) * P].bitcast(FP4X4), wu_s)
-
-        def gate(c):
-            first_layer(gate_bank(c), c, lambda a, t: wg_w[:, a, t * P : (t + 1) * P].bitcast(FP8X4), wg_s)
-
-        def hidden(c):
-            cols = slice(c * CHUNK, (c + 1) * CHUNK)
-            gated = ring.tile([P, CHUNK, PACK], F32, name="gated")
-            nc.scalar.activation(gated[:], gate_bank(c)[:].rearrange("p t j -> p j t"), TANH)
-            h_bf = ring.tile([P, CHUNK, PACK], BF16, name="h_bf", align_bytes=64)
-            nc.vector.tensor_tensor(h_bf[:], up_bank(c)[:].rearrange("p t j -> p j t"), gated[:], MULT)
-            nc.vector.quantize_mx(
-                out=h_w[:, cols].bitcast(FP8X4), scales=h_s[:, cols], in_=h_bf[:].rearrange("p j t -> p (j t)")
+        def second_layer(target, b, cols):
+            tiers = (
+                wd4_w[:].bitcast(U8)[:, 2 * b * P : 2 * (b + 1) * P].bitcast(FP4X4),
+                wd8_w[:, b * P : (b + 1) * P].bitcast(FP8X4),
             )
-
-        def down(c):
-            cols = slice(c * CHUNK, (c + 1) * CHUNK)
-            bank = up_bank(c)
-            for b in range(N // P):
-                tiers = (
-                    wd4_w[:].bitcast(U8)[:, 2 * b * P : 2 * (b + 1) * P].bitcast(FP4X4),
-                    wd8_w[:, b * P : (b + 1) * P].bitcast(FP8X4),
+            for tier in range(2):
+                nc.tensor.matmul_mx(
+                    out=target,
+                    lhsT=tiers[tier],
+                    lhsT_scale=wd_s[:, tier, :].bitcast(U8)[:, b * P : (b + 1) * P],
+                    rhs=h_w[:, cols].bitcast(FP8X4),
+                    rhs_scale=h_s[:, cols],
+                    start=(tier == 0),
+                    stop=(tier == 1),
                 )
-                for tier in range(2):
-                    nc.tensor.matmul_mx(
-                        out=bank[:, b, :],
-                        lhsT=tiers[tier],
-                        lhsT_scale=wd_s[:, tier, :].bitcast(U8)[:, b * P : (b + 1) * P],
-                        rhs=h_w[:, cols].bitcast(FP8X4),
-                        rhs_scale=h_s[:, cols],
-                        start=(tier == 0),
-                        stop=(tier == 1),
-                    )
-            staged = ring.tile([P, N // P, CHUNK], F32, name="staged")
-            nc.scalar.copy(out=staged[:], in_=bank[:])
-            nc.sync.dma_start(out=out[:, cols].rearrange("(b p) j -> p b j", p=P), in_=staged[:])
 
-        for a in range(PASSES):
-            for u in range(2):
-                cast_wg(a, u)
-        quantize_wg(0, 0, PACK)
-        quantize_wg(1, 0, 2)
-        quantize_wg(1, 2, PACK)
+        def step(kind, c, *more):
+            if kind == "load":
+                load(c, more[0])
+            elif kind == "pw":
+                nc.vector.tensor_copy(
+                    out=wu_w[:].bitcast(U16).rearrange("p a (t m) -> p a t m", t=PACK),
+                    in_=wu_w_raw[:].bitcast(U16).rearrange("p a (m t) -> p a t m", t=PACK),
+                )
+            elif kind == "ps":
+                nc.vector.tensor_copy(
+                    out=wu_s[:].rearrange("p a (t m) -> p a t m", t=PACK),
+                    in_=wu_s_raw[:].bitcast(U8).rearrange("p a (m t) -> p a t m", t=PACK),
+                )
+            elif kind == "W":
+                width = PIECES[c][1] - PIECES[c][0]
+                got[c] = held.tile([P, width], U32, name="got%d" % c, tag="v_w" if c >= HELD else "got", align_bytes=64)
+                nc.vector.tensor_copy(out=got[c][:], in_=tab_w[:].bitcast(U32).indirect(listed(c)))
+            elif kind == "P":
+                width = PIECES[c][1] - PIECES[c][0]
+                v_w[c] = held.tile([P, PASSES, 2 * width], U8, name="v_w%d" % c, tag="v_w", align_bytes=64)
+                nc.vector.tensor_copy(
+                    out=v_w[c][:].bitcast(U16).rearrange("p a (h j) -> p h a j", h=2),
+                    in_=got[c][:].bitcast(U16).rearrange("p (h j a) -> p h a j", h=2, a=PASSES),
+                )
+            elif kind == "S":
+                a = more[0]
+                width = PIECES[c][1] - PIECES[c][0]
+                if c not in v_s:
+                    v_s[c] = held.tile([P, PASSES, width], U8, name="v_s%d" % c, tag="v_s", align_bytes=64)
+                nc.vector.tensor_copy(out=v_s[c][:, a, :], in_=tab_s[:, a, :].bitcast(U8).indirect(listed(c)))
+            elif kind == "cast":
+                i, lo, hi, eng = CASTS[c]
+                a, m0, m1 = WG_PARTS[i]
+                dst = wg_bf[:, a, :, lo:hi, :].rearrange("p t m i -> p m i t")
+                src = wg_raw[i][:, :, PACK * (lo - m0) : PACK * (hi - m0)].rearrange("p i (m t) -> p m i t", t=PACK)
+                if eng == "a":
+                    nc.scalar.copy(out=dst, in_=src)
+                elif eng == "v":
+                    nc.vector.tensor_copy(out=dst, in_=src)
+                else:
+                    nc.gpsimd.tensor_scalar(dst, src, 1.0, 0.0, MULT, ADD)
+            elif kind == "q":
+                t0, t1 = more
+                cols = slice(t0 * P, t1 * P)
+                nc.vector.quantize_mx(
+                    out=wg_w[:, c, cols].bitcast(FP8X4),
+                    scales=wg_s[:, c, cols],
+                    in_=wg_bf[:, c, t0:t1, :, :].rearrange("p t m i -> p (t m i)"),
+                )
+            elif kind == "u":
+                first_layer(banks[UP_BANK[c]], c, lambda a, t: wu_w[:, a, 2 * t * P : 2 * (t + 1) * P].bitcast(FP4X4), wu_s)
+            elif kind == "g":
+                first_layer(banks[GATE_BANK[c]], c, lambda a, t: wg_w[:, a, t * P : (t + 1) * P].bitcast(FP8X4), wg_s)
+            elif kind == "t":
+                gated[c] = ring.tile([P, CHUNK, PACK], F32, name="gated")
+                nc.scalar.activation(gated[c][:], banks[GATE_BANK[c]][:].rearrange("p t j -> p j t"), TANH)
+            elif kind == "m":
+                h_bf[c] = ring.tile([P, CHUNK, PACK], BF16, name="h_bf", align_bytes=64)
+                nc.vector.tensor_tensor(h_bf[c][:], banks[UP_BANK[c]][:].rearrange("p t j -> p j t"), gated[c][:], MULT)
+            elif kind == "n":
+                cols = slice(c * CHUNK, (c + 1) * CHUNK)
+                nc.vector.quantize_mx(
+                    out=h_w[:, cols].bitcast(FP8X4), scales=h_s[:, cols], in_=h_bf[c][:].rearrange("p j t -> p (j t)")
+                )
+            elif kind == "d":
+                bank = banks[more[0]]
+                for b in range(N // P):
+                    second_layer(bank[:, b, :], b, slice(c * CHUNK, (c + 1) * CHUNK))
+            elif kind == "o":
+                bank = banks[more[0]]
+                first, count = STORES[c]
+                if c == first:
+                    staged[first] = keep.tile([P, N // P, count * CHUNK], F32, name="staged%d" % c)
+                dst = staged[first][:, :, (c - first) * CHUNK : (c - first + 1) * CHUNK]
+                if more[1] == "a":
+                    nc.scalar.copy(out=dst, in_=bank[:])
+                elif more[1] == "v":
+                    nc.vector.tensor_copy(out=dst, in_=bank[:])
+                if c == first + count - 1:
+                    stored = out[:, first * CHUNK : (first + count) * CHUNK]
+                    nc.sync.dma_start(out=stored.rearrange("(b p) j -> p b j", p=P), in_=staged[first][:])
+            elif kind == "D":
+                bank = banks[more[0]][:].rearrange("p t j -> p (t j)")
+                half = more[1]
+                second_layer(bank, c, slice(half * 512, (half + 1) * 512))
+                wide = keep.tile([P, 512], F32, name="wide%d_%d" % (c, half))
+                if more[2] == "a":
+                    nc.scalar.copy(out=wide[:], in_=bank)
+                else:
+                    nc.vector.tensor_copy(out=wide[:], in_=bank)
+                nc.sync.dma_start(out=out[c * P : (c + 1) * P, half * 512 : (half + 1) * 512], in_=wide[:])
 
-        for g in range(3):
-            gather_words(g)
-            gather_scales(g)
-            part_words(g)
-        for c in range(UP_BANKS):
-            up(c)
-        for c in range(CHUNKS):
-            gate(c)
-            if c == 2:
-                gather_words(3)
-                gather_scales(3)
-                part_words(3)
-            if c >= UP_BANKS:
-                up(c)
-            hidden(c)
-            if c >= 1:
-                down(c - 1)
-        down(CHUNKS - 1)
+        for what, q in LOADS:
+            load(what, q)
+        for s in ORDER:
+            step(*s)

@@ -25,13 +25,14 @@ CHUNK = 128
 CHUNKS = J // CHUNK
 PIECES = [(0, 256), (256, 512), (512, 768), (768, 1024)]
 WG_PARTS = [(0, 0, 64), (0, 64, 128), (1, 0, 64), (1, 64, 128)]
-CASTS = [(0, 0, 64, 'a'), (1, 64, 128, 'a'), (2, 0, 64, 'a'), (3, 64, 96, 'a'), (3, 96, 128, 'v')]
+CASTS = [(0, 0, 64, 'a'), (1, 64, 128, 'a'), (2, 0, 64, 'a'), (3, 64, 80, 'a'), (3, 80, 128, 'v')]
 STORES = [(0, 1), (1, 1), (2, 1), (3, 1), (4, 1), (5, 1), (6, 1), (7, 1)]
 UP_BANK = [0, 1, 2, 3, 4, 0, 1, 2]
 GATE_BANK = [5, 6, 7, 5, 6, 7, 5, 6]
 HELD = 4
-LOADS = [(('zero', 'wu'), 'v'), (('zero', 'tab'), 'v'), (('zero', 'wd'), 'v'), (('zero', 'warm'), 'v'), (('offs', 0), 's'), (('wuw', 0), 's'), (('tabs', 0), 's'), (('tabs', 1), 's'), (('tabs', 2), 's'), (('tabs', 3), 's'), (('wus', 0), 'a'), (('wus', 1), 'a'), (('wus', 2), 'a'), (('wus', 3), 'a'), (('tabw', 0), 's'), (('warm', 0), 'a'), (('wg', 0), 's'), (('wg', 1), 's'), (('wg', 2), 's'), (('wg', 3), 's'), (('wd4w', 0), 's'), (('wd8w', 0), 's'), (('wd4s', 0), 's'), (('wd4s', 1), 's'), (('wd4s', 2), 's'), (('wd4s', 3), 's'), (('wd8s', 0), 's'), (('wd8s', 1), 's'), (('wd8s', 2), 's'), (('wd8s', 3), 's')]
-ORDER = [('pw', 0), ('ps', 0), ('W', 0), ('P', 0), ('S', 0, 0), ('S', 0, 1), ('u', 0), ('u', 1), ('W', 1), ('P', 1), ('S', 1, 0), ('S', 1, 1), ('u', 2), ('u', 3), ('W', 2), ('P', 2), ('S', 2, 0), ('S', 2, 1), ('u', 4), ('cast', 0), ('cast', 1), ('cast', 2), ('cast', 3), ('cast', 4), ('q', 0, 0, 4), ('q', 1, 0, 1), ('q', 1, 1, 2), ('q', 1, 2, 4), ('g', 0), ('t', 0), ('m', 0), ('W', 3), ('P', 3), ('S', 3, 0), ('S', 3, 1), ('g', 1), ('t', 1), ('m', 1), ('n', 0), ('g', 2), ('t', 2), ('m', 2), ('n', 1), ('g', 3), ('t', 3), ('m', 3), ('n', 2), ('g', 4), ('t', 4), ('m', 4), ('n', 3), ('g', 5), ('u', 5), ('t', 5), ('m', 5), ('n', 4), ('g', 6), ('u', 6), ('t', 6), ('m', 6), ('n', 5), ('g', 7), ('u', 7), ('t', 7), ('m', 7), ('n', 6), ('D', 0, 3, 0, 'a'), ('D', 1, 4, 0, 'a'), ('D', 2, 7, 0, 'a'), ('D', 3, 0, 0, 'a'), ('n', 7), ('D', 0, 5, 1, 'a'), ('D', 1, 1, 1, 'v'), ('D', 2, 6, 1, 'a'), ('D', 3, 2, 1, 'v')]
+LATE = {2: ('got2', 'got0'), 3: ('wg_bf1', 'wg_raw3')}
+LOADS = [(('zero', 'tab'), 'v'), (('zero', 'wu'), 'v'), (('zero', 'wd'), 'v'), (('zero', 'warm'), 'v'), (('offs', 0), 's'), (('tabs', 0), 's'), (('tabs', 1), 's'), (('tabs', 2), 'a'), (('tabs', 3), 'a'), (('wuw', 0), 's'), (('tabw', 0), 's'), (('wus', 0), 'a'), (('wus', 1), 'a'), (('wus', 2), 'a'), (('wus', 3), 'a'), (('warm', 0), 'a'), (('wg', 0), 's'), (('wg', 1), 's'), (('wg', 2), 's'), (('wg', 3), 's'), (('wd4w', 0), 's'), (('wd8w', 0), 's'), (('wd4s', 0), 's'), (('wd4s', 1), 's'), (('wd4s', 2), 's'), (('wd4s', 3), 's'), (('wd8s', 0), 's'), (('wd8s', 1), 's'), (('wd8s', 2), 's'), (('wd8s', 3), 's')]
+ORDER = [('pw', 0), ('ps', 0), ('W', 0), ('P', 0), ('S', 0, 0), ('S', 0, 1), ('u', 0), ('u', 1), ('W', 1), ('P', 1), ('S', 1, 0), ('S', 1, 1), ('u', 2), ('u', 3), ('W', 2), ('P', 2), ('S', 2, 0), ('S', 2, 1), ('u', 4), ('cast', 0), ('cast', 1), ('cast', 2), ('cast', 3), ('cast', 4), ('q', 0, 0, 4), ('q', 1, 0, 1), ('q', 1, 1, 2), ('q', 1, 2, 4), ('W', 3), ('P', 3), ('S', 3, 0), ('S', 3, 1), ('g', 0), ('t', 0), ('m', 0), ('g', 1), ('t', 1), ('m', 1), ('n', 0), ('g', 2), ('t', 2), ('m', 2), ('n', 1), ('g', 3), ('t', 3), ('m', 3), ('n', 2), ('g', 4), ('t', 4), ('m', 4), ('n', 3), ('g', 5), ('u', 5), ('t', 5), ('m', 5), ('n', 4), ('g', 6), ('u', 6), ('t', 6), ('m', 6), ('n', 5), ('g', 7), ('u', 7), ('t', 7), ('m', 7), ('n', 6), ('D', 0, 3, 0, 'a'), ('D', 1, 4, 0, 'a'), ('D', 2, 7, 0, 'a'), ('D', 3, 0, 0, 'a'), ('n', 7), ('D', 0, 5, 1, 'a'), ('D', 1, 1, 1, 'v'), ('D', 2, 6, 1, 'a'), ('D', 3, 2, 1, 'v')]
 
 
 def tile_list_gmlpt_tanh_res_none_kernel(
@@ -47,15 +48,15 @@ def tile_list_gmlpt_tanh_res_none_kernel(
         offsets = keep.tile([P, J // 16], U16, name="offsets")
         tab_w = keep.tile([P, T], I32, name="tab_w", align_bytes=64)
         tab_s = keep.tile([P, PASSES, T // 4], I32, name="tab_s", align_bytes=64)
-        wu_w_raw = keep.tile([P, PASSES, R // 2], I32, name="wu_w_raw", align_bytes=64)
-        wu_s_raw = keep.tile([P, PASSES, R // 4], I32, name="wu_s_raw", align_bytes=64)
+        wu_w_raw = keep.tile([P, PASSES, R // 2], I32, name="wu_w_raw", tag="wu_w_raw", align_bytes=64)
+        wu_s_raw = keep.tile([P, PASSES, R // 4], I32, name="wu_s_raw", tag="wu_s_raw", align_bytes=64)
         wu_w = keep.tile([P, PASSES, 2 * R], U8, name="wu_w", align_bytes=64)
         wu_s = keep.tile([P, PASSES, R], U8, name="wu_s", align_bytes=64)
         wd4_w = keep.tile([P, N // 2], I32, name="wd4_w", align_bytes=64)
         wd8_w = keep.tile([P, N], I32, name="wd8_w", align_bytes=64)
         wd_s = keep.tile([P, 2, N // 4], I32, name="wd_s", align_bytes=64)
-        wg_raw = [keep.tile([P, PACK, PACK * (m1 - m0)], F32, name="wg_raw%d" % i, align_bytes=64) for i, (a, m0, m1) in enumerate(WG_PARTS)]
-        wg_bf = keep.tile([P, PASSES, PACK, P, PACK], BF16, name="wg_bf", align_bytes=64)
+        wg_raw = [keep.tile([P, PACK, PACK * (m1 - m0)], F32, name="wg_raw%d" % i, tag="wg_raw%d" % i, align_bytes=64) for i, (a, m0, m1) in enumerate(WG_PARTS)]
+        wg_bf = [keep.tile([P, PACK, P, PACK], BF16, name="wg_bf%d" % a, tag="wg_bf%d" % a, align_bytes=64) for a in range(PASSES)]
         wg_w = keep.tile([P, PASSES, R], U32, name="wg_w", align_bytes=64)
         wg_s = keep.tile([P, PASSES, R], U8, name="wg_s", align_bytes=64)
         got, v_w, v_s = {}, {}, {}
@@ -149,7 +150,7 @@ def tile_list_gmlpt_tanh_res_none_kernel(
                 )
             elif kind == "W":
                 width = PIECES[c][1] - PIECES[c][0]
-                got[c] = held.tile([P, width], U32, name="got%d" % c, tag="v_w" if c >= HELD else "got", align_bytes=64)
+                got[c] = keep.tile([P, width], U32, name="got%d" % c, tag=LATE.get(c, ("got%d" % c,))[0], align_bytes=64)
                 nc.vector.tensor_copy(out=got[c][:], in_=tab_w[:].bitcast(U32).indirect(listed(c)))
             elif kind == "P":
                 width = PIECES[c][1] - PIECES[c][0]
@@ -161,13 +162,15 @@ def tile_list_gmlpt_tanh_res_none_kernel(
             elif kind == "S":
                 a = more[0]
                 width = PIECES[c][1] - PIECES[c][0]
+                if c not in v_s and c in LATE:
+                    v_s[c] = keep.tile([P, PASSES, width], U8, name="v_s%d" % c, tag=LATE[c][1], align_bytes=64)
                 if c not in v_s:
                     v_s[c] = held.tile([P, PASSES, width], U8, name="v_s%d" % c, tag="v_s", align_bytes=64)
                 nc.vector.tensor_copy(out=v_s[c][:, a, :], in_=tab_s[:, a, :].bitcast(U8).indirect(listed(c)))
             elif kind == "cast":
                 i, lo, hi, eng = CASTS[c]
                 a, m0, m1 = WG_PARTS[i]
-                dst = wg_bf[:, a, :, lo:hi, :].rearrange("p t m i -> p m i t")
+                dst = wg_bf[a][:, :, lo:hi, :].rearrange("p t m i -> p m i t")
                 src = wg_raw[i][:, :, PACK * (lo - m0) : PACK * (hi - m0)].rearrange("p i (m t) -> p m i t", t=PACK)
                 if eng == "a":
                     nc.scalar.copy(out=dst, in_=src)
@@ -181,7 +184,7 @@ def tile_list_gmlpt_tanh_res_none_kernel(
                 nc.vector.quantize_mx(
                     out=wg_w[:, c, cols].bitcast(FP8X4),
                     scales=wg_s[:, c, cols],
-                    in_=wg_bf[:, c, t0:t1, :, :].rearrange("p t m i -> p (t m i)"),
+                    in_=wg_bf[c][:, t0:t1, :, :].rearrange("p t m i -> p (t m i)"),
                 )
             elif kind == "u":
                 first_layer(banks[UP_BANK[c]], c, lambda a, t: wu_w[:, a, 2 * t * P : 2 * (t + 1) * P].bitcast(FP4X4), wu_s)
@@ -225,6 +228,18 @@ def tile_list_gmlpt_tanh_res_none_kernel(
                 else:
                     nc.vector.tensor_copy(out=wide[:], in_=bank)
                 nc.sync.dma_start(out=out[c * P : (c + 1) * P, half * 512 : (half + 1) * 512], in_=wide[:])
+            elif kind == "E":
+                for part in range(2):
+                    bank = banks[more[part]]
+                    j0 = 512 + part * 256
+                    for i in range(2):
+                        second_layer(bank[:, i, :], c, slice(j0 + i * CHUNK, j0 + (i + 1) * CHUNK))
+                    narrow = keep.tile([P, 2, CHUNK], F32, name="narrow%d" % part)
+                    if part == 0:
+                        nc.scalar.copy(out=narrow[:], in_=bank[:, 0:2, :])
+                    else:
+                        nc.vector.tensor_copy(out=narrow[:], in_=bank[:, 0:2, :])
+                    nc.sync.dma_start(out=out[c * P : (c + 1) * P, j0 : j0 + 256], in_=narrow[:].rearrange("p i j -> p (i j)"))
 
         for what, q in LOADS:
             load(what, q)

@@ -15,7 +15,6 @@ FP8X4 = mybir.dt.float8_e4m3fn_x4
 FP4X4 = mybir.dt.float4_e2m1fn_x4
 TANH = mybir.ActivationFunctionType.Tanh
 MULT = mybir.AluOpType.mult
-ADD = mybir.AluOpType.add
 
 P = 128
 PACK = 4
@@ -23,16 +22,14 @@ K_PASS = P * PACK
 PASSES = K // K_PASS
 CHUNK = 128
 CHUNKS = J // CHUNK
-PIECES = [(0, 256), (256, 512), (512, 768), (768, 1024)]
-WG_PARTS = [(0, 0, 64), (0, 64, 128), (1, 0, 64), (1, 64, 128)]
-CASTS = [(0, 0, 64, 'a'), (1, 64, 128, 'a'), (2, 0, 64, 'a'), (3, 64, 80, 'a'), (3, 80, 128, 'v')]
-STORES = [(0, 1), (1, 1), (2, 1), (3, 1), (4, 1), (5, 1), (6, 1), (7, 1)]
-UP_BANK = [0, 1, 2, 3, 4, 0, 1, 2]
-GATE_BANK = [5, 6, 7, 5, 6, 7, 5, 6]
-HELD = 4
-LATE = {2: ('got2', 'got0'), 3: ('wg_bf1', 'wg_raw3')}
-LOADS = [(('zero', 'tab'), 'v'), (('zero', 'wu'), 'v'), (('zero', 'wd'), 'v'), (('zero', 'warm'), 'v'), (('offs', 0), 's'), (('tabs', 0), 's'), (('tabs', 1), 's'), (('tabs', 2), 'a'), (('tabs', 3), 'a'), (('wuw', 0), 's'), (('tabw', 0), 's'), (('wus', 0), 'a'), (('wus', 1), 'a'), (('wus', 2), 'a'), (('wus', 3), 'a'), (('warm', 0), 'a'), (('wg', 0), 's'), (('wg', 1), 's'), (('wg', 2), 's'), (('wg', 3), 's'), (('wd4w', 0), 's'), (('wd8w', 0), 's'), (('wd4s', 0), 's'), (('wd4s', 1), 's'), (('wd4s', 2), 's'), (('wd4s', 3), 's'), (('wd8s', 0), 's'), (('wd8s', 1), 's'), (('wd8s', 2), 's'), (('wd8s', 3), 's')]
-ORDER = [('pw', 0), ('ps', 0), ('W', 0), ('P', 0), ('S', 0, 0), ('S', 0, 1), ('u', 0), ('u', 1), ('W', 1), ('P', 1), ('S', 1, 0), ('S', 1, 1), ('u', 2), ('u', 3), ('W', 2), ('P', 2), ('S', 2, 0), ('S', 2, 1), ('u', 4), ('cast', 0), ('cast', 1), ('cast', 2), ('cast', 3), ('cast', 4), ('q', 0, 0, 4), ('q', 1, 0, 1), ('q', 1, 1, 2), ('q', 1, 2, 4), ('W', 3), ('P', 3), ('S', 3, 0), ('S', 3, 1), ('g', 0), ('t', 0), ('m', 0), ('g', 1), ('t', 1), ('m', 1), ('n', 0), ('g', 2), ('t', 2), ('m', 2), ('n', 1), ('g', 3), ('t', 3), ('m', 3), ('n', 2), ('g', 4), ('t', 4), ('m', 4), ('n', 3), ('g', 5), ('u', 5), ('t', 5), ('m', 5), ('n', 4), ('g', 6), ('u', 6), ('t', 6), ('m', 6), ('n', 5), ('g', 7), ('u', 7), ('t', 7), ('m', 7), ('n', 6), ('D', 0, 3, 0, 'a'), ('D', 1, 4, 0, 'a'), ('D', 2, 7, 0, 'a'), ('D', 3, 0, 0, 'a'), ('n', 7), ('D', 0, 5, 1, 'a'), ('D', 1, 1, 1, 'v'), ('D', 2, 6, 1, 'a'), ('D', 3, 2, 1, 'v')]
+PIECE = 256
+PIECES = J // PIECE
+HALF = 512
+WG_PARTS = [(a, m0, m0 + 64) for a in range(PASSES) for m0 in (0, 64)]
+UP_BANKS = 5
+GATE_BANKS = 3
+SHIFT = 16
+LAST_SPLIT = 80
 
 
 def tile_list_gmlpt_tanh_res_none_kernel(
@@ -42,86 +39,126 @@ def tile_list_gmlpt_tanh_res_none_kernel(
     with ExitStack() as ctx:
         keep = ctx.enter_context(tc.tile_pool(name="keep", bufs=1))
         ring = ctx.enter_context(tc.tile_pool(name="ring", bufs=4))
-        held = ctx.enter_context(tc.tile_pool(name="held", bufs=HELD))
         psum = ctx.enter_context(tc.psum_pool(name="psum", bufs=1))
 
         offsets = keep.tile([P, J // 16], U16, name="offsets")
         tab_w = keep.tile([P, T], I32, name="tab_w", align_bytes=64)
-        tab_s = keep.tile([P, PASSES, T // 4], I32, name="tab_s", align_bytes=64)
-        wu_w_raw = keep.tile([P, PASSES, R // 2], I32, name="wu_w_raw", tag="wu_w_raw", align_bytes=64)
+        tab_s = keep.tile([P, T // 4], I32, name="tab_s", align_bytes=64)
+        v_s = [keep.tile([P, J // 4], I32, name="v_s%d" % a, align_bytes=64) for a in range(PASSES)]
+        wu_w_raw = keep.tile([P, PASSES, R // 2], I32, name="wu_w_raw", align_bytes=64)
         wu_s_raw = keep.tile([P, PASSES, R // 4], I32, name="wu_s_raw", tag="wu_s_raw", align_bytes=64)
-        wu_w = keep.tile([P, PASSES, 2 * R], U8, name="wu_w", align_bytes=64)
+        wu_w = keep.tile([P, PASSES, R], U16, name="wu_w", align_bytes=64)
         wu_s = keep.tile([P, PASSES, R], U8, name="wu_s", align_bytes=64)
         wd4_w = keep.tile([P, N // 2], I32, name="wd4_w", align_bytes=64)
         wd8_w = keep.tile([P, N], I32, name="wd8_w", align_bytes=64)
         wd_s = keep.tile([P, 2, N // 4], I32, name="wd_s", align_bytes=64)
-        wg_raw = [keep.tile([P, PACK, PACK * (m1 - m0)], F32, name="wg_raw%d" % i, tag="wg_raw%d" % i, align_bytes=64) for i, (a, m0, m1) in enumerate(WG_PARTS)]
+        wg_raw = [keep.tile([P, PACK, PACK * (m1 - m0)], F32, name="wg_raw%d" % i, align_bytes=64) for i, (a, m0, m1) in enumerate(WG_PARTS)]
         wg_bf = [keep.tile([P, PACK, P, PACK], BF16, name="wg_bf%d" % a, tag="wg_bf%d" % a, align_bytes=64) for a in range(PASSES)]
         wg_w = keep.tile([P, PASSES, R], U32, name="wg_w", align_bytes=64)
         wg_s = keep.tile([P, PASSES, R], U8, name="wg_s", align_bytes=64)
-        got, v_w, v_s = {}, {}, {}
+        v_w = [keep.tile([P, PASSES, PIECE], U16, name="v_w%d" % g, align_bytes=64) for g in range(PIECES)]
+        h_bf = keep.tile([P, J, PACK], BF16, name="h_bf", align_bytes=64)
         h_w = keep.tile([P, J], U32, name="h_w", align_bytes=64)
         h_s = keep.tile([P, J], U8, name="h_s", align_bytes=64)
         warm = keep.tile([P, 8], F32, name="warm")
         warm_out = keep.tile([P, 8], F32, name="warm_out")
         banks = [psum.tile([P, PACK, CHUNK], F32, name="bank%d" % b) for b in range(8)]
-        staged, gated, h_bf = {}, {}, {}
-        queues = {"s": nc.sync, "a": nc.scalar, "g": nc.gpsimd}
 
-        def scale_rows(queue, tile_rows, scales, r):
-            queue.dma_start(out=tile_rows, in_=scales.bitcast(I32)[:, r:16:4, :].rearrange("a q w -> q a w"))
+        def scale_rows(tile_rows, scales, r):
+            nc.sync.dma_start(out=tile_rows, in_=scales.bitcast(I32)[:, r:16:4, :].rearrange("a q w -> q a w"))
 
-        def load(what, q):
-            queue = queues.get(q)
-            kind, i = what
-            if kind == "offs":
-                nc.sync.dma_start(offsets[:], offs)
-            elif kind == "wuw":
-                queue.dma_start(out=wu_w_raw[:], in_=wu_words.bitcast(I32).rearrange("a p w -> p a w"))
-            elif kind == "tabw":
-                queue.dma_start(out=tab_w[:], in_=tab_words[0].rearrange("p t b -> p (t b)").bitcast(I32))
-            elif kind == "wus":
-                scale_rows(queue, wu_s_raw[i:P:32, :, :], wu_scales, i)
-            elif kind == "tabs":
-                scale_rows(queue, tab_s[i:P:32, :, :], tab_scales, i)
-            elif kind == "wd4s":
-                scale_rows(queue, wd_s[i:P:32, 0:1, :], wd4_scales, i)
-            elif kind == "wd8s":
-                scale_rows(queue, wd_s[i:P:32, 1:2, :], wd8_scales, i)
-            elif kind == "wg":
-                a, m0, m1 = WG_PARTS[i]
-                rows = wg[a * K_PASS : (a + 1) * K_PASS, PACK * m0 : PACK * m1]
-                queue.dma_start(out=wg_raw[i][:], in_=rows.rearrange("(p i) r -> p i r", i=PACK))
-            elif kind == "wd4w":
-                queue.dma_start(out=wd4_w[:], in_=wd4_words[0].bitcast(I32))
-            elif kind == "wd8w":
-                queue.dma_start(out=wd8_w[:], in_=wd8_words[0].rearrange("p n b -> p (n b)").bitcast(I32))
-            elif kind == "warm":
-                nc.scalar.activation(warm_out[:], warm[:], TANH)
-            elif kind == "zero":
-                (nc.vector if q == "v" else nc.gpsimd).memset({"tab": tab_s, "wu": wu_s_raw, "wd": wd_s, "warm": warm}[i][:], 0)
+        def load_wg(i):
+            a, m0, m1 = WG_PARTS[i]
+            rows = wg[a * K_PASS : (a + 1) * K_PASS, PACK * m0 : PACK * m1]
+            nc.sync.dma_start(out=wg_raw[i][:], in_=rows.rearrange("(p i) r -> p i r", i=PACK))
 
-        def listed(g):
-            return offsets[:, PIECES[g][0] // 16 : PIECES[g][1] // 16]
+        for plane in (tab_s, warm, wu_s_raw, v_s[1], wd_s):
+            nc.vector.memset(plane[:], 0)
+        nc.scalar.activation(warm_out[:], warm[:], TANH)
+
+        nc.sync.dma_start(offsets[:], offs)
+        nc.sync.dma_start(out=wu_w_raw[:], in_=wu_words.bitcast(I32).rearrange("a p w -> p a w"))
+        for r in range(4):
+            scale_rows(tab_s[r:P:SHIFT, :], tab_scales, r)
+        nc.sync.dma_start(out=tab_w[:], in_=tab_words[0].rearrange("p t b -> p (t b)").bitcast(I32))
+        for r in range(4):
+            scale_rows(wu_s_raw[r:P:32, :, :], wu_scales, r)
+        for i in range(len(WG_PARTS)):
+            load_wg(i)
+        nc.sync.dma_start(out=wd4_w[:], in_=wd4_words[0].bitcast(I32))
+        nc.sync.dma_start(out=wd8_w[:], in_=wd8_words[0].rearrange("p n b -> p (n b)").bitcast(I32))
+        for tier, scales in enumerate((wd4_scales, wd8_scales)):
+            for r in range(4):
+                scale_rows(wd_s[r:P:32, tier : tier + 1, :], scales, r)
+
+        nc.vector.tensor_copy(out=v_s[0][:].bitcast(U8), in_=tab_s[:].bitcast(U8).indirect(offsets[:]))
+        nc.scalar.dma_start(out=v_s[1][0 : P - SHIFT, :], in_=v_s[0][SHIFT:P, :])
+
+        def gather_words(g):
+            got = got_tiles[g]
+            listed = offsets[:, g * PIECE // 16 : (g + 1) * PIECE // 16]
+            nc.vector.tensor_copy(out=got[:], in_=tab_w[:].bitcast(U32).indirect(listed))
+            nc.vector.tensor_copy(
+                out=v_w[g][:].rearrange("p a (h j) -> p h a j", h=2),
+                in_=got[:].bitcast(U16).rearrange("p (h j a) -> p h a j", h=2, a=PASSES),
+            )
 
         def first_layer(bank, c, weight, weight_scale):
-            g = [i for i, (j0, j1) in enumerate(PIECES) if j0 <= c * CHUNK < j1][0]
-            lo = c * CHUNK - PIECES[g][0]
+            g, lo = divmod(c * CHUNK, PIECE)
             for t in range(PACK):
                 for a in range(PASSES):
                     nc.tensor.matmul_mx(
                         out=bank[:, t, :],
-                        lhsT=weight(a, t),
+                        lhsT=weight[:, a, t * P : (t + 1) * P],
                         lhsT_scale=weight_scale[:, a, t * P : (t + 1) * P],
-                        rhs=v_w[g][:, a, 2 * lo : 2 * (lo + CHUNK)].bitcast(FP4X4),
-                        rhs_scale=v_s[g][:, a, lo : lo + CHUNK],
+                        rhs=v_w[g][:, a, lo : lo + CHUNK].bitcast(FP4X4),
+                        rhs_scale=v_s[a][:].bitcast(U8)[:, c * CHUNK : (c + 1) * CHUNK],
                         start=(a == 0),
                         stop=(a == PASSES - 1),
                     )
 
-        def second_layer(target, b, cols):
+        def up(c):
+            first_layer(banks[c % UP_BANKS], c, wu_w[:].bitcast(FP4X4), wu_s)
+
+        def gate_bank(c):
+            return banks[UP_BANKS + c % GATE_BANKS]
+
+        def gate(c):
+            first_layer(gate_bank(c), c, wg_w[:].bitcast(FP8X4), wg_s)
+
+        def activate(c):
+            gated = ring.tile([P, CHUNK, PACK], F32, name="gated")
+            nc.scalar.activation(gated[:], gate_bank(c)[:].rearrange("p t j -> p j t"), TANH)
+            nc.vector.tensor_tensor(
+                h_bf[:, c * CHUNK : (c + 1) * CHUNK, :], banks[c % UP_BANKS][:].rearrange("p t j -> p j t"), gated[:], MULT
+            )
+
+        def quantise_h(c0, c1):
+            cols = slice(c0 * CHUNK, c1 * CHUNK)
+            nc.vector.quantize_mx(
+                out=h_w[:, cols].bitcast(FP8X4), scales=h_s[:, cols], in_=h_bf[:, cols, :].rearrange("p j t -> p (j t)")
+            )
+
+        def round_wg(copy, i, lo, hi):
+            a, m0, m1 = WG_PARTS[i]
+            copy(
+                out=wg_bf[a][:, :, lo:hi, :].rearrange("p t m i -> p m i t"),
+                in_=wg_raw[i][:, :, PACK * (lo - m0) : PACK * (hi - m0)].rearrange("p i (m t) -> p m i t", t=PACK),
+            )
+
+        def quantise_wg(a, t0, t1):
+            cols = slice(t0 * P, t1 * P)
+            nc.vector.quantize_mx(
+                out=wg_w[:, a, cols].bitcast(FP8X4),
+                scales=wg_s[:, a, cols],
+                in_=wg_bf[a][:, t0:t1, :, :].rearrange("p t m i -> p (t m i)"),
+            )
+
+        def down(b, half, bank, engine):
+            cols = slice(half * HALF, (half + 1) * HALF)
+            target = bank[:].rearrange("p t j -> p (t j)")
             tiers = (
-                wd4_w[:].bitcast(U8)[:, 2 * b * P : 2 * (b + 1) * P].bitcast(FP4X4),
+                wd4_w[:].bitcast(U16)[:, b * P : (b + 1) * P].bitcast(FP4X4),
                 wd8_w[:, b * P : (b + 1) * P].bitcast(FP8X4),
             )
             for tier in range(2):
@@ -134,114 +171,49 @@ def tile_list_gmlpt_tanh_res_none_kernel(
                     start=(tier == 0),
                     stop=(tier == 1),
                 )
+            y = keep.tile([P, HALF], F32, name="y%d_%d" % (b, half))
+            if engine == "scalar":
+                nc.scalar.copy(out=y[:], in_=target)
+            else:
+                nc.vector.tensor_copy(out=y[:], in_=target)
+            nc.sync.dma_start(out=out[b * P : (b + 1) * P, cols], in_=y[:])
 
-        def step(kind, c, *more):
-            if kind == "load":
-                load(c, more[0])
-            elif kind == "pw":
-                nc.vector.tensor_copy(
-                    out=wu_w[:].bitcast(U16).rearrange("p a (t m) -> p a t m", t=PACK),
-                    in_=wu_w_raw[:].bitcast(U16).rearrange("p a (m t) -> p a t m", t=PACK),
-                )
-            elif kind == "ps":
-                nc.vector.tensor_copy(
-                    out=wu_s[:].rearrange("p a (t m) -> p a t m", t=PACK),
-                    in_=wu_s_raw[:].bitcast(U8).rearrange("p a (m t) -> p a t m", t=PACK),
-                )
-            elif kind == "W":
-                width = PIECES[c][1] - PIECES[c][0]
-                got[c] = keep.tile([P, width], U32, name="got%d" % c, tag=LATE.get(c, ("got%d" % c,))[0], align_bytes=64)
-                nc.vector.tensor_copy(out=got[c][:], in_=tab_w[:].bitcast(U32).indirect(listed(c)))
-            elif kind == "P":
-                width = PIECES[c][1] - PIECES[c][0]
-                v_w[c] = held.tile([P, PASSES, 2 * width], U8, name="v_w%d" % c, tag="v_w", align_bytes=64)
-                nc.vector.tensor_copy(
-                    out=v_w[c][:].bitcast(U16).rearrange("p a (h j) -> p h a j", h=2),
-                    in_=got[c][:].bitcast(U16).rearrange("p (h j a) -> p h a j", h=2, a=PASSES),
-                )
-            elif kind == "S":
-                a = more[0]
-                width = PIECES[c][1] - PIECES[c][0]
-                if c not in v_s and c in LATE:
-                    v_s[c] = keep.tile([P, PASSES, width], U8, name="v_s%d" % c, tag=LATE[c][1], align_bytes=64)
-                if c not in v_s:
-                    v_s[c] = held.tile([P, PASSES, width], U8, name="v_s%d" % c, tag="v_s", align_bytes=64)
-                nc.vector.tensor_copy(out=v_s[c][:, a, :], in_=tab_s[:, a, :].bitcast(U8).indirect(listed(c)))
-            elif kind == "cast":
-                i, lo, hi, eng = CASTS[c]
-                a, m0, m1 = WG_PARTS[i]
-                dst = wg_bf[a][:, :, lo:hi, :].rearrange("p t m i -> p m i t")
-                src = wg_raw[i][:, :, PACK * (lo - m0) : PACK * (hi - m0)].rearrange("p i (m t) -> p m i t", t=PACK)
-                if eng == "a":
-                    nc.scalar.copy(out=dst, in_=src)
-                elif eng == "v":
-                    nc.vector.tensor_copy(out=dst, in_=src)
-                else:
-                    nc.gpsimd.tensor_scalar(dst, src, 1.0, 0.0, MULT, ADD)
-            elif kind == "q":
-                t0, t1 = more
-                cols = slice(t0 * P, t1 * P)
-                nc.vector.quantize_mx(
-                    out=wg_w[:, c, cols].bitcast(FP8X4),
-                    scales=wg_s[:, c, cols],
-                    in_=wg_bf[c][:, t0:t1, :, :].rearrange("p t m i -> p (t m i)"),
-                )
-            elif kind == "u":
-                first_layer(banks[UP_BANK[c]], c, lambda a, t: wu_w[:, a, 2 * t * P : 2 * (t + 1) * P].bitcast(FP4X4), wu_s)
-            elif kind == "g":
-                first_layer(banks[GATE_BANK[c]], c, lambda a, t: wg_w[:, a, t * P : (t + 1) * P].bitcast(FP8X4), wg_s)
-            elif kind == "t":
-                gated[c] = ring.tile([P, CHUNK, PACK], F32, name="gated")
-                nc.scalar.activation(gated[c][:], banks[GATE_BANK[c]][:].rearrange("p t j -> p j t"), TANH)
-            elif kind == "m":
-                h_bf[c] = ring.tile([P, CHUNK, PACK], BF16, name="h_bf", align_bytes=64)
-                nc.vector.tensor_tensor(h_bf[c][:], banks[UP_BANK[c]][:].rearrange("p t j -> p j t"), gated[c][:], MULT)
-            elif kind == "n":
-                cols = slice(c * CHUNK, (c + 1) * CHUNK)
-                nc.vector.quantize_mx(
-                    out=h_w[:, cols].bitcast(FP8X4), scales=h_s[:, cols], in_=h_bf[c][:].rearrange("p j t -> p (j t)")
-                )
-            elif kind == "d":
-                bank = banks[more[0]]
-                for b in range(N // P):
-                    second_layer(bank[:, b, :], b, slice(c * CHUNK, (c + 1) * CHUNK))
-            elif kind == "o":
-                bank = banks[more[0]]
-                first, count = STORES[c]
-                if c == first:
-                    staged[first] = keep.tile([P, N // P, count * CHUNK], F32, name="staged%d" % c)
-                dst = staged[first][:, :, (c - first) * CHUNK : (c - first + 1) * CHUNK]
-                if more[1] == "a":
-                    nc.scalar.copy(out=dst, in_=bank[:])
-                elif more[1] == "v":
-                    nc.vector.tensor_copy(out=dst, in_=bank[:])
-                if c == first + count - 1:
-                    stored = out[:, first * CHUNK : (first + count) * CHUNK]
-                    nc.sync.dma_start(out=stored.rearrange("(b p) j -> p b j", p=P), in_=staged[first][:])
-            elif kind == "D":
-                bank = banks[more[0]][:].rearrange("p t j -> p (t j)")
-                half = more[1]
-                second_layer(bank, c, slice(half * 512, (half + 1) * 512))
-                wide = keep.tile([P, 512], F32, name="wide%d_%d" % (c, half))
-                if more[2] == "a":
-                    nc.scalar.copy(out=wide[:], in_=bank)
-                else:
-                    nc.vector.tensor_copy(out=wide[:], in_=bank)
-                nc.sync.dma_start(out=out[c * P : (c + 1) * P, half * 512 : (half + 1) * 512], in_=wide[:])
-            elif kind == "E":
-                for part in range(2):
-                    bank = banks[more[part]]
-                    j0 = 512 + part * 256
-                    for i in range(2):
-                        second_layer(bank[:, i, :], c, slice(j0 + i * CHUNK, j0 + (i + 1) * CHUNK))
-                    narrow = keep.tile([P, 2, CHUNK], F32, name="narrow%d" % part)
-                    if part == 0:
-                        nc.scalar.copy(out=narrow[:], in_=bank[:, 0:2, :])
-                    else:
-                        nc.vector.tensor_copy(out=narrow[:], in_=bank[:, 0:2, :])
-                    nc.sync.dma_start(out=out[c * P : (c + 1) * P, j0 : j0 + 256], in_=narrow[:].rearrange("p i j -> p (i j)"))
+        got_tiles = {0: keep.tile([P, PIECE], U32, name="got_first", align_bytes=64)}
+        gather_words(0)
+        nc.vector.tensor_copy(
+            out=wu_s[:].rearrange("p a (t m) -> p a t m", t=PACK),
+            in_=wu_s_raw[:].bitcast(U8).rearrange("p a (m t) -> p a t m", t=PACK),
+        )
+        nc.vector.tensor_copy(
+            out=wu_w[:].rearrange("p a (t m) -> p a t m", t=PACK),
+            in_=wu_w_raw[:].bitcast(U16).rearrange("p a (m t) -> p a t m", t=PACK),
+        )
+        got_middle = keep.tile([P, 2 * PIECE], U32, name="got_middle", tag="wu_s_raw", align_bytes=64)
+        got_tiles.update({1: got_middle[:, :PIECE], 2: got_middle[:, PIECE:]})
+        for c in range(UP_BANKS):
+            if c % 2 == 0 and c > 0:
+                gather_words(c // 2)
+            up(c)
+        for i, (a, m0, m1) in enumerate(WG_PARTS[:-1]):
+            round_wg(nc.scalar.copy, i, m0, m1)
+        round_wg(nc.scalar.copy, 3, 64, LAST_SPLIT)
+        quantise_wg(0, 0, 4)
+        round_wg(nc.vector.tensor_copy, 3, LAST_SPLIT, 128)
+        quantise_wg(1, 0, 1)
+        quantise_wg(1, 1, 2)
+        quantise_wg(1, 2, 4)
+        got_tiles[3] = keep.tile([P, PIECE], U32, name="got_last", tag="wg_bf1", align_bytes=64)
+        gather_words(3)
 
-        for what, q in LOADS:
-            load(what, q)
-        for s in ORDER:
-            step(*s)
+        for c in range(CHUNKS):
+            gate(c)
+            if c >= UP_BANKS:
+                up(c)
+            activate(c)
+            if c % 2 == 0 and c > 0:
+                quantise_h(c - 2, c)
+        for b in range(4):
+            down(b, 0, banks[(3, 4, 7, 0)[b]], "scalar")
+        quantise_h(CHUNKS - 2, CHUNKS)
+        for b in range(4):
+            down(b, 1, banks[(5, 1, 6, 2)[b]], "scalar" if b % 2 == 0 else "vector")

@@ -26,8 +26,10 @@ PIECE = 256
 PIECES = J // PIECE
 HALF = 512
 WG_PARTS = [(a, m0, m0 + 64) for a in range(PASSES) for m0 in (0, 64)]
-UP_BANKS = 5
-GATE_BANKS = 3
+UP_BANKS = 6
+GATE_BANKS = 2
+UP_BANK = (0, 1, 2, 3, 4, 5, 2, 3)
+GATE_BANK = (6, 7, 6, 7, 0, 1, 6, 7)
 SHIFT = 16
 LAST_SPLIT = 80
 
@@ -48,7 +50,7 @@ def tile_list_gmlpt_tanh_res_none_kernel(
         wu_w_raw = keep.tile([P, PASSES, R // 2], I32, name="wu_w_raw", align_bytes=64)
         wu_s_raw = keep.tile([P, PASSES, R // 4], I32, name="wu_s_raw", tag="wu_s_raw", align_bytes=64)
         wu_w = keep.tile([P, PASSES, R], U16, name="wu_w", align_bytes=64)
-        wu_s = keep.tile([P, PASSES, R], U8, name="wu_s", align_bytes=64)
+        wu_s = [keep.tile([P, R], U8, name="wu_s%d" % a, align_bytes=64) for a in range(PASSES)]
         wd4_w = keep.tile([P, N // 2], I32, name="wd4_w", align_bytes=64)
         wd8_w = keep.tile([P, N], I32, name="wd8_w", align_bytes=64)
         wd_s = keep.tile([P, 2, N // 4], I32, name="wd_s", align_bytes=64)
@@ -63,6 +65,10 @@ def tile_list_gmlpt_tanh_res_none_kernel(
         warm = keep.tile([P, 8], F32, name="warm")
         warm_out = keep.tile([P, 8], F32, name="warm_out")
         banks = [psum.tile([P, PACK, CHUNK], F32, name="bank%d" % b) for b in range(8)]
+
+        def bank_of(key):
+            kind, c = key
+            return banks[(UP_BANK if kind == "up" else GATE_BANK)[c]]
 
         def scale_rows(tile_rows, scales, r):
             nc.sync.dma_start(out=tile_rows, in_=scales.bitcast(I32)[:, r:16:4, :].rearrange("a q w -> q a w"))
@@ -83,16 +89,18 @@ def tile_list_gmlpt_tanh_res_none_kernel(
         nc.sync.dma_start(out=tab_w[:], in_=tab_words[0].rearrange("p t b -> p (t b)").bitcast(I32))
         for r in range(4):
             scale_rows(wu_s_raw[r:P:32, :, :], wu_scales, r)
-        for i in range(len(WG_PARTS)):
-            load_wg(i)
+        load_wg(0)
+        load_wg(1)
+        nc.vector.tensor_copy(out=v_s[0][:].bitcast(U8), in_=tab_s[:].bitcast(U8).indirect(offsets[:]))
+        nc.sync.dma_start(out=v_s[1][0 : P - SHIFT, :], in_=v_s[0][SHIFT:P, :])
+        load_wg(2)
+        load_wg(3)
         nc.sync.dma_start(out=wd4_w[:], in_=wd4_words[0].bitcast(I32))
         nc.sync.dma_start(out=wd8_w[:], in_=wd8_words[0].rearrange("p n b -> p (n b)").bitcast(I32))
         for tier, scales in enumerate((wd4_scales, wd8_scales)):
             for r in range(4):
                 scale_rows(wd_s[r:P:32, tier : tier + 1, :], scales, r)
 
-        nc.vector.tensor_copy(out=v_s[0][:].bitcast(U8), in_=tab_s[:].bitcast(U8).indirect(offsets[:]))
-        nc.scalar.dma_start(out=v_s[1][0 : P - SHIFT, :], in_=v_s[0][SHIFT:P, :])
 
         def gather_words(g):
             got = got_tiles[g]
@@ -103,34 +111,33 @@ def tile_list_gmlpt_tanh_res_none_kernel(
                 in_=got[:].bitcast(U16).rearrange("p (h j a) -> p h a j", h=2, a=PASSES),
             )
 
-        def first_layer(bank, c, weight, weight_scale):
+        def first_layer(bank, c, a, weight, weight_scale):
             g, lo = divmod(c * CHUNK, PIECE)
             for t in range(PACK):
-                for a in range(PASSES):
-                    nc.tensor.matmul_mx(
-                        out=bank[:, t, :],
-                        lhsT=weight[:, a, t * P : (t + 1) * P],
-                        lhsT_scale=weight_scale[:, a, t * P : (t + 1) * P],
-                        rhs=v_w[g][:, a, lo : lo + CHUNK].bitcast(FP4X4),
-                        rhs_scale=v_s[a][:].bitcast(U8)[:, c * CHUNK : (c + 1) * CHUNK],
-                        start=(a == 0),
-                        stop=(a == PASSES - 1),
-                    )
+                nc.tensor.matmul_mx(
+                    out=bank[:, t, :],
+                    lhsT=weight[:, a, t * P : (t + 1) * P],
+                    lhsT_scale=weight_scale[:, t * P : (t + 1) * P],
+                    rhs=v_w[g][:, a, lo : lo + CHUNK].bitcast(FP4X4),
+                    rhs_scale=v_s[a][:].bitcast(U8)[:, c * CHUNK : (c + 1) * CHUNK],
+                    start=(a == 0 and t == 0),
+                    stop=(a == PASSES - 1 and t == PACK - 1),
+                )
 
-        def up(c):
-            first_layer(banks[c % UP_BANKS], c, wu_w[:].bitcast(FP4X4), wu_s)
+        def up(c, a):
+            first_layer(bank_of(("up", c)), c, a, wu_w[:].bitcast(FP4X4), wu_s[a])
 
         def gate_bank(c):
-            return banks[UP_BANKS + c % GATE_BANKS]
+            return bank_of(("gate", c))
 
-        def gate(c):
-            first_layer(gate_bank(c), c, wg_w[:].bitcast(FP8X4), wg_s)
+        def gate(c, a):
+            first_layer(gate_bank(c), c, a, wg_w[:].bitcast(FP8X4), wg_s[:, a, :])
 
         def activate(c):
             gated = ring.tile([P, CHUNK, PACK], F32, name="gated")
             nc.scalar.activation(gated[:], gate_bank(c)[:].rearrange("p t j -> p j t"), TANH)
             nc.vector.tensor_tensor(
-                h_bf[:, c * CHUNK : (c + 1) * CHUNK, :], banks[c % UP_BANKS][:].rearrange("p t j -> p j t"), gated[:], MULT
+                h_bf[:, c * CHUNK : (c + 1) * CHUNK, :], bank_of(("up", c))[:].rearrange("p t j -> p j t"), gated[:], MULT
             )
 
         def quantise_h(c0, c1):
@@ -154,50 +161,55 @@ def tile_list_gmlpt_tanh_res_none_kernel(
                 in_=wg_bf[a][:, t0:t1, :, :].rearrange("p t m i -> p (t m i)"),
             )
 
-        def down(b, half, bank, engine):
-            cols = slice(half * HALF, (half + 1) * HALF)
-            target = bank[:].rearrange("p t j -> p (t j)")
-            tiers = (
-                wd4_w[:].bitcast(U16)[:, b * P : (b + 1) * P].bitcast(FP4X4),
-                wd8_w[:, b * P : (b + 1) * P].bitcast(FP8X4),
-            )
-            for tier in range(2):
-                nc.tensor.matmul_mx(
-                    out=target,
-                    lhsT=tiers[tier],
-                    lhsT_scale=wd_s[:, tier, :].bitcast(U8)[:, b * P : (b + 1) * P],
-                    rhs=h_w[:, cols].bitcast(FP8X4),
-                    rhs_scale=h_s[:, cols],
-                    start=(tier == 0),
-                    stop=(tier == 1),
+        def down(blocks, j0, j1, width, copy, whole):
+            used = banks[whole][:].rearrange("p t j -> p (t j)")[:, : len(blocks) * (j1 - j0)]
+            bank = used.rearrange("p (b j) -> p b j", b=len(blocks))
+            for i, b in enumerate(blocks):
+                tiers = (
+                    wd4_w[:].bitcast(U16)[:, b * P : (b + 1) * P].bitcast(FP4X4),
+                    wd8_w[:, b * P : (b + 1) * P].bitcast(FP8X4),
                 )
-            y = keep.tile([P, HALF], F32, name="y%d_%d" % (b, half))
-            if engine == "scalar":
-                nc.scalar.copy(out=y[:], in_=target)
-            else:
-                nc.vector.tensor_copy(out=y[:], in_=target)
-            nc.sync.dma_start(out=out[b * P : (b + 1) * P, cols], in_=y[:])
+                for j in range(j0, j1, width):
+                    for tier in range(2):
+                        nc.tensor.matmul_mx(
+                            out=bank[:, i, j - j0 : j - j0 + width],
+                            lhsT=tiers[tier],
+                            lhsT_scale=wd_s[:, tier, :].bitcast(U8)[:, b * P : (b + 1) * P],
+                            rhs=h_w[:, j : j + width].bitcast(FP8X4),
+                            rhs_scale=h_s[:, j : j + width],
+                            start=(tier == 0),
+                            stop=(tier == 1),
+                        )
+            y = keep.tile([P, len(blocks), j1 - j0], F32, name="y%d_%d" % (blocks[0], j0))
+            copy(out=y[:], in_=bank)
+            rows = out[blocks[0] * P : (blocks[-1] + 1) * P, j0:j1]
+            nc.sync.dma_start(out=rows.rearrange("(b p) j -> p b j", p=P), in_=y[:])
 
-        got_tiles = {0: keep.tile([P, PIECE], U32, name="got_first", align_bytes=64)}
+        got_tiles = {0: keep.tile([P, PIECE], U32, name="got_first", tag="got_first", align_bytes=64)}
         gather_words(0)
-        nc.vector.tensor_copy(
-            out=wu_s[:].rearrange("p a (t m) -> p a t m", t=PACK),
-            in_=wu_s_raw[:].bitcast(U8).rearrange("p a (m t) -> p a t m", t=PACK),
-        )
+        for a in range(PASSES):
+            nc.gpsimd.tensor_copy(
+                out=wu_s[a][:].rearrange("p (t m) -> p t m", t=PACK),
+                in_=wu_s_raw[:, a, :].bitcast(U8).rearrange("p (m t) -> p t m", t=PACK),
+            )
         nc.vector.tensor_copy(
             out=wu_w[:].rearrange("p a (t m) -> p a t m", t=PACK),
             in_=wu_w_raw[:].bitcast(U16).rearrange("p a (m t) -> p a t m", t=PACK),
         )
-        got_middle = keep.tile([P, 2 * PIECE], U32, name="got_middle", tag="wu_s_raw", align_bytes=64)
+        got_middle = keep.tile([P, 2 * PIECE], U32, name="got_middle", tag="got_first", align_bytes=64)
         got_tiles.update({1: got_middle[:, :PIECE], 2: got_middle[:, PIECE:]})
         for c in range(UP_BANKS):
             if c % 2 == 0 and c > 0:
                 gather_words(c // 2)
-            up(c)
+            up(c, 0)
+        for c in range(UP_BANKS):
+            up(c, 1)
         for i, (a, m0, m1) in enumerate(WG_PARTS[:-1]):
             round_wg(nc.scalar.copy, i, m0, m1)
         round_wg(nc.scalar.copy, 3, 64, LAST_SPLIT)
         quantise_wg(0, 0, 4)
+        for c in range(GATE_BANKS):
+            gate(c, 0)
         round_wg(nc.vector.tensor_copy, 3, LAST_SPLIT, 128)
         quantise_wg(1, 0, 1)
         quantise_wg(1, 1, 2)
@@ -206,14 +218,20 @@ def tile_list_gmlpt_tanh_res_none_kernel(
         gather_words(3)
 
         for c in range(CHUNKS):
-            gate(c)
+            if c >= GATE_BANKS:
+                gate(c, 0)
+            gate(c, 1)
             if c >= UP_BANKS:
-                up(c)
+                up(c, 0)
+                up(c, 1)
             activate(c)
             if c % 2 == 0 and c > 0:
                 quantise_h(c - 2, c)
+        copies = (nc.scalar.copy, nc.vector.tensor_copy)
         for b in range(4):
-            down(b, 0, banks[(3, 4, 7, 0)[b]], "scalar")
+            down([b], 0, HALF, HALF, nc.scalar.copy, (0, 1, 4, 5)[b])
         quantise_h(CHUNKS - 2, CHUNKS)
+        for i in range(2):
+            down([2 * i, 2 * i + 1], HALF, HALF + PIECE, CHUNK, copies[i], 6 + i)
         for b in range(4):
-            down(b, 1, banks[(5, 1, 6, 2)[b]], "scalar" if b % 2 == 0 else "vector")
+            down([b], HALF + PIECE, J, CHUNK, copies[b % 2], (2, 3, 0, 1)[b])

@@ -25,13 +25,12 @@ CHUNKS = J // CHUNK
 PIECE = 256
 PIECES = J // PIECE
 HALF = 512
-WG_PARTS = [(a, m0, m0 + 64) for a in range(PASSES) for m0 in (0, 64)]
-UP_BANKS = 6
-GATE_BANKS = 2
-UP_BANK = (0, 1, 2, 3, 4, 5, 2, 3)
-GATE_BANK = (6, 7, 6, 7, 0, 1, 6, 7)
+UP_BANKS = 5
+GATE_BANKS = 3
+UP_BANK = (0, 1, 2, 3, 4, 0, 1, 2)
+GATE_BANK = (5, 6, 7, 5, 6, 7, 5, 6)
 SHIFT = 16
-LAST_SPLIT = 80
+SCALAR_COLUMNS = 44
 
 
 def tile_list_gmlpt_tanh_res_none_kernel(
@@ -54,7 +53,7 @@ def tile_list_gmlpt_tanh_res_none_kernel(
         wd4_w = keep.tile([P, N // 2], I32, name="wd4_w", align_bytes=64)
         wd8_w = keep.tile([P, N], I32, name="wd8_w", align_bytes=64)
         wd_s = keep.tile([P, 2, N // 4], I32, name="wd_s", align_bytes=64)
-        wg_raw = [keep.tile([P, PACK, PACK * (m1 - m0)], F32, name="wg_raw%d" % i, align_bytes=64) for i, (a, m0, m1) in enumerate(WG_PARTS)]
+        wg_raw = [keep.tile([P, PACK, R], F32, name="wg_raw%d" % a, align_bytes=64) for a in range(PASSES)]
         wg_bf = [keep.tile([P, PACK, P, PACK], BF16, name="wg_bf%d" % a, tag="wg_bf%d" % a, align_bytes=64) for a in range(PASSES)]
         wg_w = keep.tile([P, PASSES, R], U32, name="wg_w", align_bytes=64)
         wg_s = keep.tile([P, PASSES, R], U8, name="wg_s", align_bytes=64)
@@ -73,10 +72,9 @@ def tile_list_gmlpt_tanh_res_none_kernel(
         def scale_rows(tile_rows, scales, r):
             nc.sync.dma_start(out=tile_rows, in_=scales.bitcast(I32)[:, r:16:4, :].rearrange("a q w -> q a w"))
 
-        def load_wg(i):
-            a, m0, m1 = WG_PARTS[i]
-            rows = wg[a * K_PASS : (a + 1) * K_PASS, PACK * m0 : PACK * m1]
-            nc.sync.dma_start(out=wg_raw[i][:], in_=rows.rearrange("(p i) r -> p i r", i=PACK))
+        def load_wg(a):
+            rows = wg[a * K_PASS : (a + 1) * K_PASS, :]
+            nc.sync.dma_start(out=wg_raw[a][:], in_=rows.rearrange("(p i) r -> p i r", i=PACK))
 
         for plane in (tab_s, warm, wu_s_raw, v_s[1], wd_s):
             nc.vector.memset(plane[:], 0)
@@ -90,11 +88,9 @@ def tile_list_gmlpt_tanh_res_none_kernel(
         for r in range(4):
             scale_rows(wu_s_raw[r:P:32, :, :], wu_scales, r)
         load_wg(0)
-        load_wg(1)
         nc.vector.tensor_copy(out=v_s[0][:].bitcast(U8), in_=tab_s[:].bitcast(U8).indirect(offsets[:]))
         nc.sync.dma_start(out=v_s[1][0 : P - SHIFT, :], in_=v_s[0][SHIFT:P, :])
-        load_wg(2)
-        load_wg(3)
+        load_wg(1)
         nc.sync.dma_start(out=wd4_w[:], in_=wd4_words[0].bitcast(I32))
         nc.sync.dma_start(out=wd8_w[:], in_=wd8_words[0].rearrange("p n b -> p (n b)").bitcast(I32))
         for tier, scales in enumerate((wd4_scales, wd8_scales)):
@@ -146,12 +142,12 @@ def tile_list_gmlpt_tanh_res_none_kernel(
                 out=h_w[:, cols].bitcast(FP8X4), scales=h_s[:, cols], in_=h_bf[:, cols, :].rearrange("p j t -> p (j t)")
             )
 
-        def round_wg(copy, i, lo, hi):
-            a, m0, m1 = WG_PARTS[i]
-            copy(
-                out=wg_bf[a][:, :, lo:hi, :].rearrange("p t m i -> p m i t"),
-                in_=wg_raw[i][:, :, PACK * (lo - m0) : PACK * (hi - m0)].rearrange("p i (m t) -> p m i t", t=PACK),
-            )
+        def round_wg(a):
+            for copy, lo, hi in ((nc.scalar.copy, 0, SCALAR_COLUMNS), (nc.vector.tensor_copy, SCALAR_COLUMNS, P)):
+                copy(
+                    out=wg_bf[a][:, :, lo:hi, :].rearrange("p t m i -> p m i t"),
+                    in_=wg_raw[a][:, :, PACK * lo : PACK * hi].rearrange("p i (m t) -> p m i t", t=PACK),
+                )
 
         def quantise_wg(a, t0, t1):
             cols = slice(t0 * P, t1 * P)
@@ -204,20 +200,22 @@ def tile_list_gmlpt_tanh_res_none_kernel(
             up(c, 0)
         for c in range(UP_BANKS):
             up(c, 1)
-        for i, (a, m0, m1) in enumerate(WG_PARTS[:-1]):
-            round_wg(nc.scalar.copy, i, m0, m1)
-        round_wg(nc.scalar.copy, 3, 64, LAST_SPLIT)
+        round_wg(0)
         quantise_wg(0, 0, 4)
         for c in range(GATE_BANKS):
             gate(c, 0)
-        round_wg(nc.vector.tensor_copy, 3, LAST_SPLIT, 128)
+        round_wg(1)
         quantise_wg(1, 0, 1)
         quantise_wg(1, 1, 2)
         quantise_wg(1, 2, 4)
         got_tiles[3] = keep.tile([P, PIECE], U32, name="got_last", tag="wg_bf1", align_bytes=64)
         gather_words(3)
 
+        copies = (nc.scalar.copy, nc.vector.tensor_copy)
         for c in range(CHUNKS):
+            if c == CHUNKS - 1:
+                for pair in range(2):
+                    down([2 * pair, 2 * pair + 1], 0, PIECE, CHUNK, nc.scalar.copy, 3 + pair)
             if c >= GATE_BANKS:
                 gate(c, 0)
             gate(c, 1)
@@ -227,11 +225,7 @@ def tile_list_gmlpt_tanh_res_none_kernel(
             activate(c)
             if c % 2 == 0 and c > 0:
                 quantise_h(c - 2, c)
-        copies = (nc.scalar.copy, nc.vector.tensor_copy)
-        for b in range(4):
-            down([b], 0, HALF, HALF, nc.scalar.copy, (0, 1, 4, 5)[b])
         quantise_h(CHUNKS - 2, CHUNKS)
-        for i in range(2):
-            down([2 * i, 2 * i + 1], HALF, HALF + PIECE, CHUNK, copies[i], 6 + i)
-        for b in range(4):
-            down([b], HALF + PIECE, J, CHUNK, copies[b % 2], (2, 3, 0, 1)[b])
+        for i, whole in enumerate((7, 0, 5, 3, 1, 4, 6, 7, 2, 0, 5, 3)):
+            g, b = divmod(4 + i, 4)
+            down([b], g * PIECE, (g + 1) * PIECE, CHUNK, copies[g > 1 and b % 2], whole)

@@ -25,10 +25,7 @@ CHUNKS = J // CHUNK
 PIECE = 256
 PIECES = J // PIECE
 HALF = 512
-UP_BANKS = 5
-GATE_BANKS = 3
-UP_BANK = (0, 1, 2, 3, 4, 0, 1, 2)
-GATE_BANK = (5, 6, 7, 5, 6, 7, 5, 6)
+AHEAD = 4
 SHIFT = 16
 SCALAR_COLUMNS = 44
 
@@ -61,13 +58,11 @@ def tile_list_gmlpt_tanh_res_none_kernel(
         h_bf = keep.tile([P, J, PACK], BF16, name="h_bf", align_bytes=64)
         h_w = keep.tile([P, J], U32, name="h_w", align_bytes=64)
         h_s = keep.tile([P, J], U8, name="h_s", align_bytes=64)
-        warm = keep.tile([P, 8], F32, name="warm")
-        warm_out = keep.tile([P, 8], F32, name="warm_out")
         banks = [psum.tile([P, PACK, CHUNK], F32, name="bank%d" % b) for b in range(8)]
 
         def bank_of(key):
             kind, c = key
-            return banks[(UP_BANK if kind == "up" else GATE_BANK)[c]]
+            return banks[c % AHEAD + (0 if kind == "up" else AHEAD)]
 
         def scale_rows(tile_rows, scales, r):
             nc.sync.dma_start(out=tile_rows, in_=scales.bitcast(I32)[:, r:16:4, :].rearrange("a q w -> q a w"))
@@ -76,9 +71,8 @@ def tile_list_gmlpt_tanh_res_none_kernel(
             rows = wg[a * K_PASS : (a + 1) * K_PASS, :]
             nc.sync.dma_start(out=wg_raw[a][:], in_=rows.rearrange("(p i) r -> p i r", i=PACK))
 
-        for plane in (tab_s, warm, wu_s_raw, v_s[1], wd_s):
+        for plane in (tab_s, wu_s_raw, v_s[1], wd_s):
             nc.vector.memset(plane[:], 0)
-        nc.scalar.activation(warm_out[:], warm[:], TANH)
 
         nc.sync.dma_start(offsets[:], offs)
         nc.sync.dma_start(out=wu_w_raw[:], in_=wu_words.bitcast(I32).rearrange("a p w -> p a w"))
@@ -129,12 +123,18 @@ def tile_list_gmlpt_tanh_res_none_kernel(
         def gate(c, a):
             first_layer(gate_bank(c), c, a, wg_w[:].bitcast(FP8X4), wg_s[:, a, :])
 
+        gated = {}
+
         def activate(c):
-            gated = ring.tile([P, CHUNK, PACK], F32, name="gated")
-            nc.scalar.activation(gated[:], gate_bank(c)[:].rearrange("p t j -> p j t"), TANH)
+            gated[c] = ring.tile([P, CHUNK, PACK], F32, name="gated")
+            nc.scalar.activation(gated[c][:], gate_bank(c)[:].rearrange("p t j -> p j t"), TANH)
+
+        def multiply(c):
             nc.vector.tensor_tensor(
-                h_bf[:, c * CHUNK : (c + 1) * CHUNK, :], bank_of(("up", c))[:].rearrange("p t j -> p j t"), gated[:], MULT
+                h_bf[:, c * CHUNK : (c + 1) * CHUNK, :], bank_of(("up", c))[:].rearrange("p t j -> p j t"), gated[c][:], MULT
             )
+            if c % 2 == 0 and c > 0:
+                quantise_h(c - 2, c)
 
         def quantise_h(c0, c1):
             cols = slice(c0 * CHUNK, c1 * CHUNK)
@@ -194,15 +194,14 @@ def tile_list_gmlpt_tanh_res_none_kernel(
         )
         got_middle = keep.tile([P, 2 * PIECE], U32, name="got_middle", tag="got_first", align_bytes=64)
         got_tiles.update({1: got_middle[:, :PIECE], 2: got_middle[:, PIECE:]})
-        for c in range(UP_BANKS):
-            if c % 2 == 0 and c > 0:
-                gather_words(c // 2)
-            up(c, 0)
-        for c in range(UP_BANKS):
-            up(c, 1)
+        gather_words(1)
+        for a in range(PASSES):
+            for c in range(AHEAD):
+                up(c, a)
+        gather_words(2)
         round_wg(0)
         quantise_wg(0, 0, 4)
-        for c in range(GATE_BANKS):
+        for c in range(AHEAD):
             gate(c, 0)
         round_wg(1)
         quantise_wg(1, 0, 1)
@@ -212,20 +211,20 @@ def tile_list_gmlpt_tanh_res_none_kernel(
         gather_words(3)
 
         copies = (nc.scalar.copy, nc.vector.tensor_copy)
-        for c in range(CHUNKS):
-            if c == CHUNKS - 1:
-                for pair in range(2):
-                    down([2 * pair, 2 * pair + 1], 0, PIECE, CHUNK, nc.scalar.copy, 3 + pair)
-            if c >= GATE_BANKS:
-                gate(c, 0)
+        for c in range(AHEAD):
             gate(c, 1)
-            if c >= UP_BANKS:
-                up(c, 0)
-                up(c, 1)
             activate(c)
-            if c % 2 == 0 and c > 0:
-                quantise_h(c - 2, c)
+            multiply(c)
+        for c in range(AHEAD, CHUNKS + 1):
+            if c < CHUNKS:
+                gate(c, 0)
+                gate(c, 1)
+                activate(c)
+            if c > AHEAD:
+                up(c - 1, 0)
+                up(c - 1, 1)
+                multiply(c - 1)
         quantise_h(CHUNKS - 2, CHUNKS)
-        for i, whole in enumerate((7, 0, 5, 3, 1, 4, 6, 7, 2, 0, 5, 3)):
-            g, b = divmod(4 + i, 4)
-            down([b], g * PIECE, (g + 1) * PIECE, CHUNK, copies[g > 1 and b % 2], whole)
+        for i in range(8):
+            half, b = divmod(i, 4)
+            down([b], half * HALF, (half + 1) * HALF, HALF, copies[half and b % 2], (4, 5, 6, 0, 7, 1, 2, 3)[i])

@@ -25,9 +25,10 @@ CHUNKS = J // CHUNK
 PIECE = 256
 PIECES = J // PIECE
 HALF = 512
+WG_PARTS = [(a, m0, m0 + 64) for a in range(PASSES) for m0 in (0, 64)]
 AHEAD = 4
 SHIFT = 16
-SCALAR_COLUMNS = 44
+LAST_SPLIT = 80
 
 
 def tile_list_gmlpt_tanh_res_none_kernel(
@@ -50,7 +51,7 @@ def tile_list_gmlpt_tanh_res_none_kernel(
         wd4_w = keep.tile([P, N // 2], I32, name="wd4_w", align_bytes=64)
         wd8_w = keep.tile([P, N], I32, name="wd8_w", align_bytes=64)
         wd_s = keep.tile([P, 2, N // 4], I32, name="wd_s", align_bytes=64)
-        wg_raw = [keep.tile([P, PACK, R], F32, name="wg_raw%d" % a, align_bytes=64) for a in range(PASSES)]
+        wg_raw = [keep.tile([P, PACK, PACK * (m1 - m0)], F32, name="wg_raw%d" % i, align_bytes=64) for i, (a, m0, m1) in enumerate(WG_PARTS)]
         wg_bf = [keep.tile([P, PACK, P, PACK], BF16, name="wg_bf%d" % a, tag="wg_bf%d" % a, align_bytes=64) for a in range(PASSES)]
         wg_w = keep.tile([P, PASSES, R], U32, name="wg_w", align_bytes=64)
         wg_s = keep.tile([P, PASSES, R], U8, name="wg_s", align_bytes=64)
@@ -67,9 +68,10 @@ def tile_list_gmlpt_tanh_res_none_kernel(
         def scale_rows(tile_rows, scales, r):
             nc.sync.dma_start(out=tile_rows, in_=scales.bitcast(I32)[:, r:16:4, :].rearrange("a q w -> q a w"))
 
-        def load_wg(a):
-            rows = wg[a * K_PASS : (a + 1) * K_PASS, :]
-            nc.sync.dma_start(out=wg_raw[a][:], in_=rows.rearrange("(p i) r -> p i r", i=PACK))
+        def load_wg(i):
+            a, m0, m1 = WG_PARTS[i]
+            rows = wg[a * K_PASS : (a + 1) * K_PASS, PACK * m0 : PACK * m1]
+            nc.sync.dma_start(out=wg_raw[i][:], in_=rows.rearrange("(p i) r -> p i r", i=PACK))
 
         for plane in (tab_s, wu_s_raw, v_s[1], wd_s):
             nc.vector.memset(plane[:], 0)
@@ -82,9 +84,11 @@ def tile_list_gmlpt_tanh_res_none_kernel(
         for r in range(4):
             scale_rows(wu_s_raw[r:P:32, :, :], wu_scales, r)
         load_wg(0)
+        load_wg(1)
         nc.vector.tensor_copy(out=v_s[0][:].bitcast(U8), in_=tab_s[:].bitcast(U8).indirect(offsets[:]))
         nc.sync.dma_start(out=v_s[1][0 : P - SHIFT, :], in_=v_s[0][SHIFT:P, :])
-        load_wg(1)
+        load_wg(2)
+        load_wg(3)
         nc.sync.dma_start(out=wd4_w[:], in_=wd4_words[0].bitcast(I32))
         nc.sync.dma_start(out=wd8_w[:], in_=wd8_words[0].rearrange("p n b -> p (n b)").bitcast(I32))
         for tier, scales in enumerate((wd4_scales, wd8_scales)):
@@ -93,7 +97,7 @@ def tile_list_gmlpt_tanh_res_none_kernel(
 
 
         def gather_words(g):
-            got = got_tiles[g]
+            got = keep.tile([P, PIECE], U32, name="got%d" % g, tag="got" if g < PIECES - 1 else "wg_bf1", align_bytes=64)
             listed = offsets[:, g * PIECE // 16 : (g + 1) * PIECE // 16]
             nc.vector.tensor_copy(out=got[:], in_=tab_w[:].bitcast(U32).indirect(listed))
             nc.vector.tensor_copy(
@@ -142,12 +146,12 @@ def tile_list_gmlpt_tanh_res_none_kernel(
                 out=h_w[:, cols].bitcast(FP8X4), scales=h_s[:, cols], in_=h_bf[:, cols, :].rearrange("p j t -> p (j t)")
             )
 
-        def round_wg(a):
-            for copy, lo, hi in ((nc.scalar.copy, 0, SCALAR_COLUMNS), (nc.vector.tensor_copy, SCALAR_COLUMNS, P)):
-                copy(
-                    out=wg_bf[a][:, :, lo:hi, :].rearrange("p t m i -> p m i t"),
-                    in_=wg_raw[a][:, :, PACK * lo : PACK * hi].rearrange("p i (m t) -> p m i t", t=PACK),
-                )
+        def round_wg(copy, i, lo, hi):
+            a, m0, m1 = WG_PARTS[i]
+            copy(
+                out=wg_bf[a][:, :, lo:hi, :].rearrange("p t m i -> p m i t"),
+                in_=wg_raw[i][:, :, PACK * (lo - m0) : PACK * (hi - m0)].rearrange("p i (m t) -> p m i t", t=PACK),
+            )
 
         def quantise_wg(a, t0, t1):
             cols = slice(t0 * P, t1 * P)
@@ -181,7 +185,6 @@ def tile_list_gmlpt_tanh_res_none_kernel(
             rows = out[blocks[0] * P : (blocks[-1] + 1) * P, j0:j1]
             nc.sync.dma_start(out=rows.rearrange("(b p) j -> p b j", p=P), in_=y[:])
 
-        got_tiles = {0: keep.tile([P, PIECE], U32, name="got_first", tag="got_first", align_bytes=64)}
         gather_words(0)
         for a in range(PASSES):
             nc.gpsimd.tensor_copy(
@@ -192,22 +195,21 @@ def tile_list_gmlpt_tanh_res_none_kernel(
             out=wu_w[:].rearrange("p a (t m) -> p a t m", t=PACK),
             in_=wu_w_raw[:].bitcast(U16).rearrange("p a (m t) -> p a t m", t=PACK),
         )
-        got_middle = keep.tile([P, 2 * PIECE], U32, name="got_middle", tag="got_first", align_bytes=64)
-        got_tiles.update({1: got_middle[:, :PIECE], 2: got_middle[:, PIECE:]})
         gather_words(1)
         for a in range(PASSES):
             for c in range(AHEAD):
                 up(c, a)
         gather_words(2)
-        round_wg(0)
+        for i, (a, m0, m1) in enumerate(WG_PARTS[:-1]):
+            round_wg(nc.scalar.copy, i, m0, m1)
+        round_wg(nc.scalar.copy, 3, 64, LAST_SPLIT)
         quantise_wg(0, 0, 4)
         for c in range(AHEAD):
             gate(c, 0)
-        round_wg(1)
+        round_wg(nc.vector.tensor_copy, 3, LAST_SPLIT, 128)
         quantise_wg(1, 0, 1)
         quantise_wg(1, 1, 2)
         quantise_wg(1, 2, 4)
-        got_tiles[3] = keep.tile([P, PIECE], U32, name="got_last", tag="wg_bf1", align_bytes=64)
         gather_words(3)
 
         copies = (nc.scalar.copy, nc.vector.tensor_copy)
@@ -220,11 +222,13 @@ def tile_list_gmlpt_tanh_res_none_kernel(
                 gate(c, 0)
                 gate(c, 1)
                 activate(c)
+            else:
+                down([0], 0, HALF, HALF, nc.scalar.copy, AHEAD)
             if c > AHEAD:
                 up(c - 1, 0)
                 up(c - 1, 1)
                 multiply(c - 1)
         quantise_h(CHUNKS - 2, CHUNKS)
-        for i in range(8):
+        for i in range(1, 8):
             half, b = divmod(i, 4)
             down([b], half * HALF, (half + 1) * HALF, HALF, copies[half and b % 2], (4, 5, 6, 0, 7, 1, 2, 3)[i])

@@ -28,7 +28,7 @@ HALF = 512
 WG_PARTS = [(a, m0, m0 + 64) for a in range(PASSES) for m0 in (0, 64)]
 AHEAD = 4
 SHIFT = 16
-LAST_SPLIT = 80
+SCALAR_COLUMNS = 24
 
 
 def tile_list_gmlpt_tanh_res_none_kernel(
@@ -135,7 +135,7 @@ def tile_list_gmlpt_tanh_res_none_kernel(
 
         def multiply(c):
             nc.vector.tensor_tensor(
-                h_bf[:, c * CHUNK : (c + 1) * CHUNK, :], bank_of(("up", c))[:].rearrange("p t j -> p j t"), gated[c][:], MULT
+                h_bf[:, c * CHUNK : (c + 1) * CHUNK, :], ub_first[:] if c == 0 else bank_of(("up", c))[:].rearrange("p t j -> p j t"), gated[c][:], MULT
             )
             if c % 2 == 0 and c > 0:
                 quantise_h(c - 2, c)
@@ -200,13 +200,19 @@ def tile_list_gmlpt_tanh_res_none_kernel(
             for c in range(AHEAD):
                 up(c, a)
         gather_words(2)
-        for i, (a, m0, m1) in enumerate(WG_PARTS[:-1]):
-            round_wg(nc.scalar.copy, i, m0, m1)
-        round_wg(nc.scalar.copy, 3, 64, LAST_SPLIT)
+        ub_first = keep.tile([P, CHUNK, PACK], F32, name="ub_first")
+        for i, (a, m0, m1) in enumerate(WG_PARTS):
+            if i == len(WG_PARTS) - 1:
+                nc.scalar.copy(out=ub_first[:], in_=banks[0][:].rearrange("p t j -> p j t"))
+            round_wg(nc.scalar.copy, i, m0, m1 if a == 0 else m0 + SCALAR_COLUMNS)
         quantise_wg(0, 0, 4)
         for c in range(AHEAD):
             gate(c, 0)
-        round_wg(nc.vector.tensor_copy, 3, LAST_SPLIT, 128)
+        up(AHEAD, 0)
+        up(AHEAD, 1)
+        for i, (a, m0, m1) in enumerate(WG_PARTS):
+            if a == 1:
+                round_wg(nc.vector.tensor_copy, i, m0 + SCALAR_COLUMNS, m1)
         quantise_wg(1, 0, 1)
         quantise_wg(1, 1, 2)
         quantise_wg(1, 2, 4)
@@ -224,9 +230,10 @@ def tile_list_gmlpt_tanh_res_none_kernel(
                 activate(c)
             else:
                 down([0], 0, HALF, HALF, nc.scalar.copy, AHEAD)
-            if c > AHEAD:
+            if c > AHEAD + 1:
                 up(c - 1, 0)
                 up(c - 1, 1)
+            if c > AHEAD:
                 multiply(c - 1)
         quantise_h(CHUNKS - 2, CHUNKS)
         for i in range(1, 8):

@@ -29,6 +29,7 @@ WG_PARTS = [(a, m0, m0 + 64) for a in range(PASSES) for m0 in (0, 64)]
 AHEAD = 4
 SHIFT = 16
 SCALAR_COLUMNS = 24
+WARM = 4
 
 
 def tile_list_gmlpt_tanh_res_none_kernel(
@@ -185,6 +186,16 @@ def tile_list_gmlpt_tanh_res_none_kernel(
             rows = out[blocks[0] * P : (blocks[-1] + 1) * P, j0:j1]
             nc.sync.dma_start(out=rows.rearrange("(b p) j -> p b j", p=P), in_=y[:])
 
+        for w in range(WARM):
+            nc.tensor.matmul_mx(
+                out=banks[7][:].rearrange("p t j -> p (t j)"),
+                lhsT=wu_w_raw[:, 0, :].bitcast(U16)[:, 0:P].bitcast(FP4X4),
+                lhsT_scale=tab_s[:].bitcast(U8)[:, 0:P],
+                rhs=wu_w_raw[:, 0, :].bitcast(U16).bitcast(FP4X4),
+                rhs_scale=tab_s[:].bitcast(U8)[:, 0:HALF],
+                start=True,
+                stop=True,
+            )
         gather_words(0)
         for a in range(PASSES):
             nc.gpsimd.tensor_copy(

@@ -25,11 +25,11 @@ CHUNKS = J // CHUNK
 PIECE = 256
 PIECES = J // PIECE
 HALF = 512
-WG_PARTS = [(a, m0, m0 + 64) for a in range(PASSES) for m0 in (0, 64)]
-AHEAD = 4
+WG_PARTS = [(0, 0, 64), (0, 64, 128), (1, 0, 48), (1, 48, 96), (1, 96, 128)]
 SHIFT = 16
-SCALAR_COLUMNS = 24
-WARM = 4
+SPANS = [(0, 1024)]
+SCALAR_COLUMNS = (64, 64, 48, 0, 0)
+WARM = 2
 
 
 def tile_list_gmlpt_tanh_res_none_kernel(
@@ -38,33 +38,37 @@ def tile_list_gmlpt_tanh_res_none_kernel(
     nc = tc.nc
     with ExitStack() as ctx:
         keep = ctx.enter_context(tc.tile_pool(name="keep", bufs=1))
-        ring = ctx.enter_context(tc.tile_pool(name="ring", bufs=4))
+        ring = ctx.enter_context(tc.tile_pool(name="ring", bufs=8))
         psum = ctx.enter_context(tc.psum_pool(name="psum", bufs=1))
 
         offsets = keep.tile([P, J // 16], U16, name="offsets")
         tab_w = keep.tile([P, T], I32, name="tab_w", align_bytes=64)
         tab_s = keep.tile([P, T // 4], I32, name="tab_s", align_bytes=64)
-        v_s = [keep.tile([P, J // 4], I32, name="v_s%d" % a, align_bytes=64) for a in range(PASSES)]
+        moved = [keep.tile([P, (j1 - j0) // 4], I32, name="moved%d" % j0, align_bytes=64) for j0, j1 in SPANS]
         wu_w_raw = keep.tile([P, PASSES, R // 2], I32, name="wu_w_raw", align_bytes=64)
-        wu_s_raw = keep.tile([P, PASSES, R // 4], I32, name="wu_s_raw", tag="wu_s_raw", align_bytes=64)
+        wu_s_raw = keep.tile([P, PASSES, R // 4], I32, name="wu_s_raw", align_bytes=64)
         wu_w = keep.tile([P, PASSES, R], U16, name="wu_w", align_bytes=64)
         wu_s = [keep.tile([P, R], U8, name="wu_s%d" % a, align_bytes=64) for a in range(PASSES)]
         wd4_w = keep.tile([P, N // 2], I32, name="wd4_w", align_bytes=64)
         wd8_w = keep.tile([P, N], I32, name="wd8_w", align_bytes=64)
         wd_s = keep.tile([P, 2, N // 4], I32, name="wd_s", align_bytes=64)
-        wg_raw = [keep.tile([P, PACK, PACK * (m1 - m0)], F32, name="wg_raw%d" % i, align_bytes=64) for i, (a, m0, m1) in enumerate(WG_PARTS)]
+        wg_raw = [keep.tile([P, PACK, PACK * (m1 - m0)], F32, name="wg_raw%d" % i, tag="wg_raw%d" % i, align_bytes=64) for i, (a, m0, m1) in enumerate(WG_PARTS)]
         wg_bf = [keep.tile([P, PACK, P, PACK], BF16, name="wg_bf%d" % a, tag="wg_bf%d" % a, align_bytes=64) for a in range(PASSES)]
         wg_w = keep.tile([P, PASSES, R], U32, name="wg_w", align_bytes=64)
         wg_s = keep.tile([P, PASSES, R], U8, name="wg_s", align_bytes=64)
         v_w = [keep.tile([P, PASSES, PIECE], U16, name="v_w%d" % g, align_bytes=64) for g in range(PIECES)]
+        ub_first = keep.tile([P, 2, PIECE, 2], F32, name="ub_first", align_bytes=64)
         h_bf = keep.tile([P, J, PACK], BF16, name="h_bf", align_bytes=64)
         h_w = keep.tile([P, J], U32, name="h_w", align_bytes=64)
         h_s = keep.tile([P, J], U8, name="h_s", align_bytes=64)
-        banks = [psum.tile([P, PACK, CHUNK], F32, name="bank%d" % b) for b in range(8)]
+        banks = [psum.tile([P, HALF], F32, name="bank%d" % b) for b in range(8)]
+        picked = {}
 
-        def bank_of(key):
-            kind, c = key
-            return banks[c % AHEAD + (0 if kind == "up" else AHEAD)]
+        def up_bank(c):
+            return banks[(0, 1, 2, 3, 4, 5, 2, 3)[c]]
+
+        def gate_bank(c):
+            return banks[(4, 5, 6, 7, 0, 1, 6, 7)[c]]
 
         def scale_rows(tile_rows, scales, r):
             nc.sync.dma_start(out=tile_rows, in_=scales.bitcast(I32)[:, r:16:4, :].rearrange("a q w -> q a w"))
@@ -74,72 +78,79 @@ def tile_list_gmlpt_tanh_res_none_kernel(
             rows = wg[a * K_PASS : (a + 1) * K_PASS, PACK * m0 : PACK * m1]
             nc.sync.dma_start(out=wg_raw[i][:], in_=rows.rearrange("(p i) r -> p i r", i=PACK))
 
-        for plane in (tab_s, wu_s_raw, v_s[1], wd_s):
-            nc.vector.memset(plane[:], 0)
+        def gather_scales(s, tag):
+            j0, j1 = SPANS[s]
+            picked[s] = keep.tile([P, (j1 - j0) // 4], I32, name="picked%d" % s, tag=tag, align_bytes=64)
+            nc.vector.tensor_copy(out=picked[s][:].bitcast(U8), in_=tab_s[:].bitcast(U8).indirect(offsets[:, j0 // 16 : j1 // 16]))
 
-        nc.sync.dma_start(offsets[:], offs)
-        nc.sync.dma_start(out=wu_w_raw[:], in_=wu_words.bitcast(I32).rearrange("a p w -> p a w"))
-        for r in range(4):
-            scale_rows(tab_s[r:P:SHIFT, :], tab_scales, r)
-        nc.sync.dma_start(out=tab_w[:], in_=tab_words[0].rearrange("p t b -> p (t b)").bitcast(I32))
-        for r in range(4):
-            scale_rows(wu_s_raw[r:P:32, :, :], wu_scales, r)
-        load_wg(0)
-        load_wg(1)
-        nc.vector.tensor_copy(out=v_s[0][:].bitcast(U8), in_=tab_s[:].bitcast(U8).indirect(offsets[:]))
-        nc.sync.dma_start(out=v_s[1][0 : P - SHIFT, :], in_=v_s[0][SHIFT:P, :])
-        load_wg(2)
-        load_wg(3)
-        nc.sync.dma_start(out=wd4_w[:], in_=wd4_words[0].bitcast(I32))
-        nc.sync.dma_start(out=wd8_w[:], in_=wd8_words[0].rearrange("p n b -> p (n b)").bitcast(I32))
-        for tier, scales in enumerate((wd4_scales, wd8_scales)):
-            for r in range(4):
-                scale_rows(wd_s[r:P:32, tier : tier + 1, :], scales, r)
+        def shift(s):
+            for p0, p1 in ((0, 64), (64, 96), (96, 100)):
+                nc.sync.dma_start(out=moved[s][p0:p1, :], in_=picked[s][p0 + SHIFT : p1 + SHIFT, :])
 
+        def table_scale(a, j0, j1):
+            s = 0 if j0 < SPANS[0][1] else 1
+            plane = picked[s] if a == 0 else moved[s]
+            return plane[:].bitcast(U8)[:, j0 - SPANS[s][0] : j1 - SPANS[s][0]]
 
-        def gather_words(g):
-            got = keep.tile([P, PIECE], U32, name="got%d" % g, tag="got" if g < PIECES - 1 else "wg_bf1", align_bytes=64)
-            listed = offsets[:, g * PIECE // 16 : (g + 1) * PIECE // 16]
+        def gather_words(g0, g1, tag):
+            got = keep.tile([P, (g1 - g0) * PIECE], U32, name="got%d" % g0, tag=tag, align_bytes=64)
+            listed = offsets[:, g0 * PIECE // 16 : g1 * PIECE // 16]
             nc.vector.tensor_copy(out=got[:], in_=tab_w[:].bitcast(U32).indirect(listed))
-            nc.vector.tensor_copy(
-                out=v_w[g][:].rearrange("p a (h j) -> p h a j", h=2),
-                in_=got[:].bitcast(U16).rearrange("p (h j a) -> p h a j", h=2, a=PASSES),
-            )
+            for g in range(g0, g1):
+                words = got[:, (g - g0) * PIECE : (g - g0 + 1) * PIECE]
+                nc.vector.tensor_copy(
+                    out=v_w[g][:].rearrange("p a (h j) -> p h a j", h=2),
+                    in_=words.bitcast(U16).rearrange("p (h j a) -> p h a j", h=2, a=PASSES),
+                )
 
-        def first_layer(bank, c, a, weight, weight_scale):
+        def first_layer(bank, c, a, weight, weight_scale, first):
             g, lo = divmod(c * CHUNK, PIECE)
             for t in range(PACK):
                 nc.tensor.matmul_mx(
-                    out=bank[:, t, :],
+                    out=bank[:, t * CHUNK : (t + 1) * CHUNK],
                     lhsT=weight[:, a, t * P : (t + 1) * P],
                     lhsT_scale=weight_scale[:, t * P : (t + 1) * P],
                     rhs=v_w[g][:, a, lo : lo + CHUNK].bitcast(FP4X4),
-                    rhs_scale=v_s[a][:].bitcast(U8)[:, c * CHUNK : (c + 1) * CHUNK],
-                    start=(a == 0 and t == 0),
-                    stop=(a == PASSES - 1 and t == PACK - 1),
+                    rhs_scale=table_scale(a, c * CHUNK, (c + 1) * CHUNK),
+                    start=(a == first and t == 0),
+                    stop=(a != first and t == PACK - 1),
                 )
 
         def up(c, a):
-            first_layer(bank_of(("up", c)), c, a, wu_w[:].bitcast(FP4X4), wu_s[a])
+            first_layer(up_bank(c), c, a, wu_w[:].bitcast(FP4X4), wu_s[a], 1)
 
-        def gate_bank(c):
-            return bank_of(("gate", c))
+        def up_first_piece(a):
+            for t in range(PACK):
+                nc.tensor.matmul_mx(
+                    out=banks[t // 2][:, t % 2 * PIECE : (t % 2 + 1) * PIECE],
+                    lhsT=wu_w[:].bitcast(FP4X4)[:, a, t * P : (t + 1) * P],
+                    lhsT_scale=wu_s[a][:, t * P : (t + 1) * P],
+                    rhs=v_w[0][:, a, :].bitcast(FP4X4),
+                    rhs_scale=table_scale(a, 0, PIECE),
+                    start=(a == 0 and t % 2 == 0),
+                    stop=(a == PASSES - 1 and t % 2 == 1),
+                )
 
         def gate(c, a):
-            first_layer(gate_bank(c), c, a, wg_w[:].bitcast(FP8X4), wg_s[:, a, :])
+            first_layer(gate_bank(c), c, a, wg_w[:].bitcast(FP8X4), wg_s[:, a, :], 0)
 
         gated = {}
 
         def activate(c):
             gated[c] = ring.tile([P, CHUNK, PACK], F32, name="gated")
-            nc.scalar.activation(gated[c][:], gate_bank(c)[:].rearrange("p t j -> p j t"), TANH)
+            nc.scalar.activation(gated[c][:], gate_bank(c)[:].rearrange("p (t j) -> p j t", t=PACK), TANH)
 
         def multiply(c):
-            nc.vector.tensor_tensor(
-                h_bf[:, c * CHUNK : (c + 1) * CHUNK, :], ub_first[:] if c == 0 else bank_of(("up", c))[:].rearrange("p t j -> p j t"), gated[c][:], MULT
-            )
-            if c % 2 == 0 and c > 0:
-                quantise_h(c - 2, c)
+            rows = h_bf[:, c * CHUNK : (c + 1) * CHUNK, :]
+            if c < 2:
+                nc.vector.tensor_tensor(
+                    rows.rearrange("p j (u e) -> p j u e", u=2),
+                    ub_first[:, :, c * CHUNK : (c + 1) * CHUNK, :].rearrange("p u j e -> p j u e"),
+                    gated[c][:].rearrange("p j (u e) -> p j u e", u=2),
+                    MULT,
+                )
+            else:
+                nc.vector.tensor_tensor(rows, up_bank(c)[:].rearrange("p (t j) -> p j t", t=PACK), gated[c][:], MULT)
 
         def quantise_h(c0, c1):
             cols = slice(c0 * CHUNK, c1 * CHUNK)
@@ -154,6 +165,16 @@ def tile_list_gmlpt_tanh_res_none_kernel(
                 in_=wg_raw[i][:, :, PACK * (lo - m0) : PACK * (hi - m0)].rearrange("p i (m t) -> p m i t", t=PACK),
             )
 
+        def round_on_scalar(i):
+            a, m0, m1 = WG_PARTS[i]
+            if SCALAR_COLUMNS[i] > 0:
+                round_wg(nc.scalar.copy, i, m0, m0 + SCALAR_COLUMNS[i])
+
+        def round_on_vector(i):
+            a, m0, m1 = WG_PARTS[i]
+            if m0 + SCALAR_COLUMNS[i] < m1:
+                round_wg(nc.vector.tensor_copy, i, m0 + SCALAR_COLUMNS[i], m1)
+
         def quantise_wg(a, t0, t1):
             cols = slice(t0 * P, t1 * P)
             nc.vector.quantize_mx(
@@ -162,41 +183,55 @@ def tile_list_gmlpt_tanh_res_none_kernel(
                 in_=wg_bf[a][:, t0:t1, :, :].rearrange("p t m i -> p (t m i)"),
             )
 
-        def down(blocks, j0, j1, width, copy, whole):
-            used = banks[whole][:].rearrange("p t j -> p (t j)")[:, : len(blocks) * (j1 - j0)]
-            bank = used.rearrange("p (b j) -> p b j", b=len(blocks))
-            for i, b in enumerate(blocks):
-                tiers = (
-                    wd4_w[:].bitcast(U16)[:, b * P : (b + 1) * P].bitcast(FP4X4),
-                    wd8_w[:, b * P : (b + 1) * P].bitcast(FP8X4),
+        def down(b, half, copy, bank):
+            tiers = (
+                wd4_w[:].bitcast(U16)[:, b * P : (b + 1) * P].bitcast(FP4X4),
+                wd8_w[:, b * P : (b + 1) * P].bitcast(FP8X4),
+            )
+            cols = slice(half * HALF, (half + 1) * HALF)
+            for tier in range(2):
+                nc.tensor.matmul_mx(
+                    out=bank[:],
+                    lhsT=tiers[tier],
+                    lhsT_scale=wd_s[:, tier, :].bitcast(U8)[:, b * P : (b + 1) * P],
+                    rhs=h_w[:, cols].bitcast(FP8X4),
+                    rhs_scale=h_s[:, cols],
+                    start=(tier == 0),
+                    stop=(tier == 1),
                 )
-                for j in range(j0, j1, width):
-                    for tier in range(2):
-                        nc.tensor.matmul_mx(
-                            out=bank[:, i, j - j0 : j - j0 + width],
-                            lhsT=tiers[tier],
-                            lhsT_scale=wd_s[:, tier, :].bitcast(U8)[:, b * P : (b + 1) * P],
-                            rhs=h_w[:, j : j + width].bitcast(FP8X4),
-                            rhs_scale=h_s[:, j : j + width],
-                            start=(tier == 0),
-                            stop=(tier == 1),
-                        )
-            y = keep.tile([P, len(blocks), j1 - j0], F32, name="y%d_%d" % (blocks[0], j0))
-            copy(out=y[:], in_=bank)
-            rows = out[blocks[0] * P : (blocks[-1] + 1) * P, j0:j1]
-            nc.sync.dma_start(out=rows.rearrange("(b p) j -> p b j", p=P), in_=y[:])
+            y = keep.tile([P, HALF], F32, name="y%d_%d" % (b, half))
+            copy(out=y[:], in_=bank[:])
+            nc.sync.dma_start(out=out[b * P : (b + 1) * P, cols], in_=y[:])
+
+        for plane in (tab_s, wu_s_raw, moved[0], wd_s):
+            nc.vector.memset(plane[:], 0)
+
+        nc.sync.dma_start(offsets[:], offs)
+        nc.sync.dma_start(out=wu_w_raw[:], in_=wu_words.bitcast(I32).rearrange("a p w -> p a w"))
+        for r in range(4):
+            scale_rows(tab_s[r:P:SHIFT, :], tab_scales, r)
+        nc.sync.dma_start(out=tab_w[:], in_=tab_words[0].rearrange("p t b -> p (t b)").bitcast(I32))
+        for r in range(4):
+            scale_rows(wu_s_raw[r:P:32, :, :], wu_scales, r)
+        load_wg(0)
+        load_wg(1)
+        gather_scales(0, "picked0")
+        shift(0)
+        load_wg(2)
+        load_wg(3)
+        load_wg(4)
 
         for w in range(WARM):
             nc.tensor.matmul_mx(
-                out=banks[7][:].rearrange("p t j -> p (t j)"),
+                out=banks[7][:],
                 lhsT=wu_w_raw[:, 0, :].bitcast(U16)[:, 0:P].bitcast(FP4X4),
-                lhsT_scale=tab_s[:].bitcast(U8)[:, 0:P],
+                lhsT_scale=table_scale(0, 0, P),
                 rhs=wu_w_raw[:, 0, :].bitcast(U16).bitcast(FP4X4),
-                rhs_scale=tab_s[:].bitcast(U8)[:, 0:HALF],
+                rhs_scale=table_scale(0, 0, HALF),
                 start=True,
                 stop=True,
             )
-        gather_words(0)
+        gather_words(0, 1, "got")
         for a in range(PASSES):
             nc.gpsimd.tensor_copy(
                 out=wu_s[a][:].rearrange("p (t m) -> p t m", t=PACK),
@@ -206,47 +241,53 @@ def tile_list_gmlpt_tanh_res_none_kernel(
             out=wu_w[:].rearrange("p a (t m) -> p a t m", t=PACK),
             in_=wu_w_raw[:].bitcast(U16).rearrange("p a (m t) -> p a t m", t=PACK),
         )
-        gather_words(1)
+        gather_words(1, 3, "got")
         for a in range(PASSES):
-            for c in range(AHEAD):
-                up(c, a)
-        gather_words(2)
-        ub_first = keep.tile([P, CHUNK, PACK], F32, name="ub_first")
-        for i, (a, m0, m1) in enumerate(WG_PARTS):
-            if i == len(WG_PARTS) - 1:
-                nc.scalar.copy(out=ub_first[:], in_=banks[0][:].rearrange("p t j -> p j t"))
-            round_wg(nc.scalar.copy, i, m0, m1 if a == 0 else m0 + SCALAR_COLUMNS)
+            up_first_piece(a)
+        for c in (2, 3):
+            up(c, 1)
+            up(c, 0)
+        nc.sync.dma_start(out=wd4_w[:], in_=wd4_words[0].bitcast(I32))
+        nc.sync.dma_start(out=wd8_w[:], in_=wd8_words[0].rearrange("p n b -> p (n b)").bitcast(I32))
+        for tier, scales in enumerate((wd4_scales, wd8_scales)):
+            for r in range(4):
+                scale_rows(wd_s[r:P:32, tier : tier + 1, :], scales, r)
+
+        round_on_scalar(0)
+        round_on_scalar(1)
+        round_on_scalar(2)
+        for u in range(2):
+            nc.scalar.copy(out=ub_first[:, u, :, :], in_=banks[u][:].rearrange("p (e j) -> p j e", e=2))
         quantise_wg(0, 0, 4)
-        for c in range(AHEAD):
+        for c in range(6):
             gate(c, 0)
-        up(AHEAD, 0)
-        up(AHEAD, 1)
-        for i, (a, m0, m1) in enumerate(WG_PARTS):
-            if a == 1:
-                round_wg(nc.vector.tensor_copy, i, m0 + SCALAR_COLUMNS, m1)
+        round_on_vector(3)
+        round_on_vector(4)
         quantise_wg(1, 0, 1)
         quantise_wg(1, 1, 2)
         quantise_wg(1, 2, 4)
-        gather_words(3)
+        gather_words(3, 4, "wg_bf1")
 
-        copies = (nc.scalar.copy, nc.vector.tensor_copy)
-        for c in range(AHEAD):
+        for c in range(6):
             gate(c, 1)
+        for c in range(CHUNKS):
+            if c >= 6:
+                up(c, 1)
+                up(c, 0)
             activate(c)
+            if c < 2:
+                up(c + 4, 1)
+                up(c + 4, 0)
+            elif c < 4:
+                gate(c + 4, 0)
+                gate(c + 4, 1)
+            if c == CHUNKS - 1:
+                down(0, 0, nc.scalar.copy, banks[0])
             multiply(c)
-        for c in range(AHEAD, CHUNKS + 1):
-            if c < CHUNKS:
-                gate(c, 0)
-                gate(c, 1)
-                activate(c)
-            else:
-                down([0], 0, HALF, HALF, nc.scalar.copy, AHEAD)
-            if c > AHEAD + 1:
-                up(c - 1, 0)
-                up(c - 1, 1)
-            if c > AHEAD:
-                multiply(c - 1)
-        quantise_h(CHUNKS - 2, CHUNKS)
+            if c % 2 == 0 and c > 0:
+                quantise_h(c - 2, c)
+        quantise_h(6, 8)
+        copies = (nc.scalar.copy, nc.vector.tensor_copy)
         for i in range(1, 8):
             half, b = divmod(i, 4)
-            down([b], half * HALF, (half + 1) * HALF, HALF, copies[half and b % 2], (4, 5, 6, 0, 7, 1, 2, 3)[i])
+            down(b, half, copies[half and b % 2], banks[(0, 1, 6, 7, 4, 5, 2, 3)[i]])

@@ -29,7 +29,6 @@ WG_PARTS = [(0, 0, 64), (0, 64, 128), (1, 0, 48), (1, 48, 96), (1, 96, 128)]
 SHIFT = 16
 SPANS = [(0, 1024)]
 SCALAR_COLUMNS = (64, 64, 48, 0, 0)
-WARM = 2
 
 
 def tile_list_gmlpt_tanh_res_none_kernel(
@@ -221,16 +220,6 @@ def tile_list_gmlpt_tanh_res_none_kernel(
         load_wg(3)
         load_wg(4)
 
-        for w in range(WARM):
-            nc.tensor.matmul_mx(
-                out=banks[7][:],
-                lhsT=wu_w_raw[:, 0, :].bitcast(U16)[:, 0:P].bitcast(FP4X4),
-                lhsT_scale=table_scale(0, 0, P),
-                rhs=wu_w_raw[:, 0, :].bitcast(U16).bitcast(FP4X4),
-                rhs_scale=table_scale(0, 0, HALF),
-                start=True,
-                stop=True,
-            )
         gather_words(0, 1, "got")
         for a in range(PASSES):
             nc.gpsimd.tensor_copy(
@@ -284,9 +273,13 @@ def tile_list_gmlpt_tanh_res_none_kernel(
             if c == CHUNKS - 1:
                 down(0, 0, nc.scalar.copy, banks[0])
             multiply(c)
-            if c % 2 == 0 and c > 0:
+            if c in (2, 4):
                 quantise_h(c - 2, c)
-        quantise_h(6, 8)
+            if c == 6:
+                quantise_h(4, 6)
+            if c == 7:
+                quantise_h(6, 7)
+        quantise_h(7, 8)
         copies = (nc.scalar.copy, nc.vector.tensor_copy)
         for i in range(1, 8):
             half, b = divmod(i, 4)

@@ -27,7 +27,8 @@ PIECES = J // PIECE
 HALF = 512
 WG_PARTS = [(0, 0, 64), (0, 64, 128), (1, 0, 48), (1, 48, 96), (1, 96, 128)]
 SHIFT = 16
-SPANS = [(0, 1024)]
+WARM_UPS = 4
+SPANS = [(0, 256), (256, 1024)]
 SCALAR_COLUMNS = (64, 64, 48, 0, 0)
 
 
@@ -38,6 +39,7 @@ def tile_list_gmlpt_tanh_res_none_kernel(
     with ExitStack() as ctx:
         keep = ctx.enter_context(tc.tile_pool(name="keep", bufs=1))
         ring = ctx.enter_context(tc.tile_pool(name="ring", bufs=8))
+        lane = ctx.enter_context(tc.tile_pool(name="lane", bufs=1))
         psum = ctx.enter_context(tc.psum_pool(name="psum", bufs=1))
 
         offsets = keep.tile([P, J // 16], U16, name="offsets")
@@ -45,7 +47,7 @@ def tile_list_gmlpt_tanh_res_none_kernel(
         tab_s = keep.tile([P, T // 4], I32, name="tab_s", align_bytes=64)
         moved = [keep.tile([P, (j1 - j0) // 4], I32, name="moved%d" % j0, align_bytes=64) for j0, j1 in SPANS]
         wu_w_raw = keep.tile([P, PASSES, R // 2], I32, name="wu_w_raw", align_bytes=64)
-        wu_s_raw = keep.tile([P, PASSES, R // 4], I32, name="wu_s_raw", align_bytes=64)
+        wu_s_raw = keep.tile([P, PASSES, R // 4], I32, name="wu_s_raw", tag="wu_s_raw", align_bytes=64)
         wu_w = keep.tile([P, PASSES, R], U16, name="wu_w", align_bytes=64)
         wu_s = [keep.tile([P, R], U8, name="wu_s%d" % a, align_bytes=64) for a in range(PASSES)]
         wd4_w = keep.tile([P, N // 2], I32, name="wd4_w", align_bytes=64)
@@ -56,7 +58,7 @@ def tile_list_gmlpt_tanh_res_none_kernel(
         wg_w = keep.tile([P, PASSES, R], U32, name="wg_w", align_bytes=64)
         wg_s = keep.tile([P, PASSES, R], U8, name="wg_s", align_bytes=64)
         v_w = [keep.tile([P, PASSES, PIECE], U16, name="v_w%d" % g, align_bytes=64) for g in range(PIECES)]
-        ub_first = keep.tile([P, 2, PIECE, 2], F32, name="ub_first", align_bytes=64)
+        ub_first = [keep.tile([P, 2, PIECE, 2], F32, name="ub_first%d" % g, align_bytes=64) for g in range(2)]
         h_bf = keep.tile([P, J, PACK], BF16, name="h_bf", align_bytes=64)
         h_w = keep.tile([P, J], U32, name="h_w", align_bytes=64)
         h_s = keep.tile([P, J], U8, name="h_s", align_bytes=64)
@@ -64,10 +66,10 @@ def tile_list_gmlpt_tanh_res_none_kernel(
         picked = {}
 
         def up_bank(c):
-            return banks[(0, 1, 2, 3, 4, 5, 2, 3)[c]]
+            return banks[(0, 1, 2, 3, 4, 5, 0, 1)[c]]
 
         def gate_bank(c):
-            return banks[(4, 5, 6, 7, 0, 1, 6, 7)[c]]
+            return banks[(6, 7, 0, 1, 2, 3, 6, 7)[c]]
 
         def scale_rows(tile_rows, scales, r):
             nc.sync.dma_start(out=tile_rows, in_=scales.bitcast(I32)[:, r:16:4, :].rearrange("a q w -> q a w"))
@@ -77,30 +79,36 @@ def tile_list_gmlpt_tanh_res_none_kernel(
             rows = wg[a * K_PASS : (a + 1) * K_PASS, PACK * m0 : PACK * m1]
             nc.sync.dma_start(out=wg_raw[i][:], in_=rows.rearrange("(p i) r -> p i r", i=PACK))
 
-        def gather_scales(s, tag):
+        def gather_scales(s, tile):
             j0, j1 = SPANS[s]
-            picked[s] = keep.tile([P, (j1 - j0) // 4], I32, name="picked%d" % s, tag=tag, align_bytes=64)
+            picked[s] = tile
             nc.vector.tensor_copy(out=picked[s][:].bitcast(U8), in_=tab_s[:].bitcast(U8).indirect(offsets[:, j0 // 16 : j1 // 16]))
 
         def shift(s):
-            for p0, p1 in ((0, 64), (64, 96), (96, 100)):
+            for p0, p1 in (((0, P - SHIFT),), ((0, 64), (64, 96), (96, 100)))[s]:
                 nc.sync.dma_start(out=moved[s][p0:p1, :], in_=picked[s][p0 + SHIFT : p1 + SHIFT, :])
 
         def table_scale(a, j0, j1):
-            s = 0 if j0 < SPANS[0][1] else 1
+            s = min(j0 // PIECE, 1)
             plane = picked[s] if a == 0 else moved[s]
             return plane[:].bitcast(U8)[:, j0 - SPANS[s][0] : j1 - SPANS[s][0]]
 
-        def gather_words(g0, g1, tag):
-            got = keep.tile([P, (g1 - g0) * PIECE], U32, name="got%d" % g0, tag=tag, align_bytes=64)
-            listed = offsets[:, g0 * PIECE // 16 : g1 * PIECE // 16]
+        def gather_words(g, got, count=1):
+            listed = offsets[:, g * PIECE // 16 : (g + count) * PIECE // 16]
             nc.vector.tensor_copy(out=got[:], in_=tab_w[:].bitcast(U32).indirect(listed))
-            for g in range(g0, g1):
-                words = got[:, (g - g0) * PIECE : (g - g0 + 1) * PIECE]
-                nc.vector.tensor_copy(
-                    out=v_w[g][:].rearrange("p a (h j) -> p h a j", h=2),
-                    in_=words.bitcast(U16).rearrange("p (h j a) -> p h a j", h=2, a=PASSES),
-                )
+            return got[:]
+
+        def part(g, got):
+            nc.vector.tensor_copy(
+                out=v_w[g][:].rearrange("p a (h j) -> p h a j", h=2),
+                in_=got.bitcast(U16).rearrange("p (h j a) -> p h a j", h=2, a=PASSES),
+            )
+
+        def kept_plane(s):
+            return keep.tile([P, (SPANS[s][1] - SPANS[s][0]) // 4], I32, name="picked%d" % s, align_bytes=64)
+
+        def lane_tile(name, dtype, columns, offset):
+            return lane.tile([P, columns], dtype, name=name, offset=offset, align_bytes=64)
 
         def first_layer(bank, c, a, weight, weight_scale, first):
             g, lo = divmod(c * CHUNK, PIECE)
@@ -118,16 +126,16 @@ def tile_list_gmlpt_tanh_res_none_kernel(
         def up(c, a):
             first_layer(up_bank(c), c, a, wu_w[:].bitcast(FP4X4), wu_s[a], 1)
 
-        def up_first_piece(a):
+        def up_piece(g, a):
             for t in range(PACK):
                 nc.tensor.matmul_mx(
-                    out=banks[t // 2][:, t % 2 * PIECE : (t % 2 + 1) * PIECE],
+                    out=banks[2 * g + t // 2][:, t % 2 * PIECE : (t % 2 + 1) * PIECE],
                     lhsT=wu_w[:].bitcast(FP4X4)[:, a, t * P : (t + 1) * P],
                     lhsT_scale=wu_s[a][:, t * P : (t + 1) * P],
-                    rhs=v_w[0][:, a, :].bitcast(FP4X4),
-                    rhs_scale=table_scale(a, 0, PIECE),
-                    start=(a == 0 and t % 2 == 0),
-                    stop=(a == PASSES - 1 and t % 2 == 1),
+                    rhs=v_w[g][:, a, :].bitcast(FP4X4),
+                    rhs_scale=table_scale(a, g * PIECE, (g + 1) * PIECE),
+                    start=(a == g and t % 2 == 0),
+                    stop=(a != g and t % 2 == 1),
                 )
 
         def gate(c, a):
@@ -141,10 +149,10 @@ def tile_list_gmlpt_tanh_res_none_kernel(
 
         def multiply(c):
             rows = h_bf[:, c * CHUNK : (c + 1) * CHUNK, :]
-            if c < 2:
+            if c < 4:
                 nc.vector.tensor_tensor(
                     rows.rearrange("p j (u e) -> p j u e", u=2),
-                    ub_first[:, :, c * CHUNK : (c + 1) * CHUNK, :].rearrange("p u j e -> p j u e"),
+                    ub_first[c // 2][:, :, c % 2 * CHUNK : (c % 2 + 1) * CHUNK, :].rearrange("p u j e -> p j u e"),
                     gated[c][:].rearrange("p j (u e) -> p j u e", u=2),
                     MULT,
                 )
@@ -202,7 +210,7 @@ def tile_list_gmlpt_tanh_res_none_kernel(
             copy(out=y[:], in_=bank[:])
             nc.sync.dma_start(out=out[b * P : (b + 1) * P, cols], in_=y[:])
 
-        for plane in (tab_s, wu_s_raw, moved[0], wd_s):
+        for plane in (tab_s, wu_s_raw, moved[0], moved[1], wd_s):
             nc.vector.memset(plane[:], 0)
 
         nc.sync.dma_start(offsets[:], offs)
@@ -213,14 +221,26 @@ def tile_list_gmlpt_tanh_res_none_kernel(
         for r in range(4):
             scale_rows(wu_s_raw[r:P:32, :, :], wu_scales, r)
         load_wg(0)
-        load_wg(1)
-        gather_scales(0, "picked0")
+        gather_scales(0, kept_plane(0))
         shift(0)
+        load_wg(1)
+        gather_scales(1, kept_plane(1))
+        shift(1)
+        for i in range(WARM_UPS):
+            nc.tensor.matmul_mx(
+                out=banks[7][:],
+                lhsT=wu_w_raw[:, 0, :].bitcast(U16)[:, 0:P].bitcast(FP4X4),
+                lhsT_scale=picked[0][:].bitcast(U8)[:, 0:P],
+                rhs=wu_w_raw[:, 1, :].bitcast(U16).bitcast(FP4X4),
+                rhs_scale=tab_s[:].bitcast(U8)[:, 0:HALF],
+                start=True,
+                stop=True,
+            )
         load_wg(2)
         load_wg(3)
         load_wg(4)
 
-        gather_words(0, 1, "got")
+        part(0, gather_words(0, lane_tile("got0", U32, PIECE, 0)))
         for a in range(PASSES):
             nc.gpsimd.tensor_copy(
                 out=wu_s[a][:].rearrange("p (t m) -> p t m", t=PACK),
@@ -230,10 +250,13 @@ def tile_list_gmlpt_tanh_res_none_kernel(
             out=wu_w[:].rearrange("p a (t m) -> p a t m", t=PACK),
             in_=wu_w_raw[:].bitcast(U16).rearrange("p a (m t) -> p a t m", t=PACK),
         )
-        gather_words(1, 3, "got")
-        for a in range(PASSES):
-            up_first_piece(a)
-        for c in (2, 3):
+        got12 = gather_words(1, lane_tile("got12", U32, 2 * PIECE, 0), 2)
+        part(1, got12[:, 0:PIECE])
+        part(2, got12[:, PIECE : 2 * PIECE])
+        for g in range(2):
+            up_piece(g, g)
+            up_piece(g, 1 - g)
+        for c in (4, 5):
             up(c, 1)
             up(c, 0)
         nc.sync.dma_start(out=wd4_w[:], in_=wd4_words[0].bitcast(I32))
@@ -245,33 +268,33 @@ def tile_list_gmlpt_tanh_res_none_kernel(
         round_on_scalar(0)
         round_on_scalar(1)
         round_on_scalar(2)
-        for u in range(2):
-            nc.scalar.copy(out=ub_first[:, u, :, :], in_=banks[u][:].rearrange("p (e j) -> p j e", e=2))
+        for b in range(4):
+            nc.scalar.copy(out=ub_first[b // 2][:, b % 2, :, :], in_=banks[b][:].rearrange("p (e j) -> p j e", e=2))
         quantise_wg(0, 0, 4)
-        for c in range(6):
+        for c in range(4):
             gate(c, 0)
         round_on_vector(3)
         round_on_vector(4)
         quantise_wg(1, 0, 1)
         quantise_wg(1, 1, 2)
         quantise_wg(1, 2, 4)
-        gather_words(3, 4, "wg_bf1")
+        part(3, gather_words(3, keep.tile([P, PIECE], U32, name="got3", tag="wg_bf1", align_bytes=64)))
 
-        for c in range(6):
+        for c in range(4):
+            gate(c, 1)
+        for c in (4, 5):
+            gate(c, 0)
             gate(c, 1)
         for c in range(CHUNKS):
-            if c >= 6:
-                up(c, 1)
-                up(c, 0)
             activate(c)
             if c < 2:
+                gate(c + 6, 0)
+                gate(c + 6, 1)
+            elif c < 4:
                 up(c + 4, 1)
                 up(c + 4, 0)
-            elif c < 4:
-                gate(c + 4, 0)
-                gate(c + 4, 1)
             if c == CHUNKS - 1:
-                down(0, 0, nc.scalar.copy, banks[0])
+                down(0, 0, nc.scalar.copy, banks[2])
             multiply(c)
             if c in (2, 4):
                 quantise_h(c - 2, c)
@@ -283,4 +306,4 @@ def tile_list_gmlpt_tanh_res_none_kernel(
         copies = (nc.scalar.copy, nc.vector.tensor_copy)
         for i in range(1, 8):
             half, b = divmod(i, 4)
-            down(b, half, copies[half and b % 2], banks[(0, 1, 6, 7, 4, 5, 2, 3)[i]])
+            down(b, half, copies[half and b % 2], banks[(2, 3, 6, 7, 4, 5, 0, 1)[i]])

@@ -25,11 +25,11 @@ CHUNKS = J // CHUNK
 PIECE = 256
 PIECES = J // PIECE
 HALF = 512
-WG_PARTS = [(0, 0, 64), (0, 64, 128), (1, 0, 48), (1, 48, 96), (1, 96, 128)]
+WG_PARTS = [(0, 0, 80), (0, 80, 128), (1, 0, 48), (1, 48, 96), (1, 96, 128)]
 SHIFT = 16
 WARM_UPS = 4
-SPANS = [(0, 256), (256, 1024)]
-SCALAR_COLUMNS = (64, 64, 48, 0, 0)
+SPANS = [(0, 512), (512, 1024)]
+SCALAR_COLUMNS = (80, 48, 48, 0, 0)
 
 
 def tile_list_gmlpt_tanh_res_none_kernel(
@@ -89,7 +89,7 @@ def tile_list_gmlpt_tanh_res_none_kernel(
                 nc.sync.dma_start(out=moved[s][p0:p1, :], in_=picked[s][p0 + SHIFT : p1 + SHIFT, :])
 
         def table_scale(a, j0, j1):
-            s = min(j0 // PIECE, 1)
+            s = j0 // HALF
             plane = picked[s] if a == 0 else moved[s]
             return plane[:].bitcast(U8)[:, j0 - SPANS[s][0] : j1 - SPANS[s][0]]
 
@@ -139,7 +139,7 @@ def tile_list_gmlpt_tanh_res_none_kernel(
                 )
 
         def gate(c, a):
-            first_layer(gate_bank(c), c, a, wg_w[:].bitcast(FP8X4), wg_s[:, a, :], 0)
+            first_layer(gate_bank(c), c, a, wg_w[:].bitcast(FP8X4), wg_s[:, a, :], 0 if c < 4 else 1)
 
         gated = {}
 
@@ -250,9 +250,8 @@ def tile_list_gmlpt_tanh_res_none_kernel(
             out=wu_w[:].rearrange("p a (t m) -> p a t m", t=PACK),
             in_=wu_w_raw[:].bitcast(U16).rearrange("p a (m t) -> p a t m", t=PACK),
         )
-        got12 = gather_words(1, lane_tile("got12", U32, 2 * PIECE, 0), 2)
-        part(1, got12[:, 0:PIECE])
-        part(2, got12[:, PIECE : 2 * PIECE])
+        part(1, gather_words(1, lane_tile("got1", U32, PIECE, 0)))
+        part(2, gather_words(2, lane_tile("got2", U32, PIECE, 0)))
         for g in range(2):
             up_piece(g, g)
             up_piece(g, 1 - g)
@@ -275,21 +274,19 @@ def tile_list_gmlpt_tanh_res_none_kernel(
             gate(c, 0)
         round_on_vector(3)
         round_on_vector(4)
-        quantise_wg(1, 0, 1)
-        quantise_wg(1, 1, 2)
-        quantise_wg(1, 2, 4)
+        quantise_wg(1, 0, 4)
         part(3, gather_words(3, keep.tile([P, PIECE], U32, name="got3", tag="wg_bf1", align_bytes=64)))
 
         for c in range(4):
             gate(c, 1)
         for c in (4, 5):
-            gate(c, 0)
             gate(c, 1)
+            gate(c, 0)
         for c in range(CHUNKS):
             activate(c)
             if c < 2:
-                gate(c + 6, 0)
                 gate(c + 6, 1)
+                gate(c + 6, 0)
             elif c < 4:
                 up(c + 4, 1)
                 up(c + 4, 0)

from contextlib import ExitStack

import concourse.mybir as mybir

K, R, N, T, J = 1024, 512, 512, 2048, 1024
FLOPS = 2 * (2 * K * R * J + 2 * R * N * J)

F32 = mybir.dt.float32
BF16 = mybir.dt.bfloat16
I32 = mybir.dt.int32
U32 = mybir.dt.uint32
U16 = mybir.dt.uint16
U8 = mybir.dt.uint8
FP8X4 = mybir.dt.float8_e4m3fn_x4
FP4X4 = mybir.dt.float4_e2m1fn_x4
TANH = mybir.ActivationFunctionType.Tanh
MULT = mybir.AluOpType.mult

P = 128
PACK = 4
K_PASS = P * PACK
PASSES = K // K_PASS
CHUNK = 128
CHUNKS = J // CHUNK
PIECE = 256
PIECES = J // PIECE
HALF = 512
WG_PARTS = [(0, 0, 80), (0, 80, 128), (1, 0, 48), (1, 48, 96), (1, 96, 128)]
SHIFT = 16
WARM_UPS = 4
SPANS = [(0, 512), (512, 1024)]
SCALAR_COLUMNS = (80, 48, 48, 0, 0)


def tile_list_gmlpt_tanh_res_none_kernel(
    tc, tab_words, tab_scales, wg, wu_words, wu_scales, wd4_words, wd4_scales, wd8_words, wd8_scales, offs, out
):
    nc = tc.nc
    with ExitStack() as ctx:
        keep = ctx.enter_context(tc.tile_pool(name="keep", bufs=1))
        ring = ctx.enter_context(tc.tile_pool(name="ring", bufs=8))
        lane = ctx.enter_context(tc.tile_pool(name="lane", bufs=1))
        psum = ctx.enter_context(tc.psum_pool(name="psum", bufs=1))

        offsets = keep.tile([P, J // 16], U16, name="offsets")
        tab_w = keep.tile([P, T], I32, name="tab_w", align_bytes=64)
        tab_s = keep.tile([P, T // 4], I32, name="tab_s", align_bytes=64)
        moved = [keep.tile([P, (j1 - j0) // 4], I32, name="moved%d" % j0, align_bytes=64) for j0, j1 in SPANS]
        wu_w_raw = keep.tile([P, PASSES, R // 2], I32, name="wu_w_raw", align_bytes=64)
        wu_s_raw = keep.tile([P, PASSES, R // 4], I32, name="wu_s_raw", tag="wu_s_raw", align_bytes=64)
        wu_w = keep.tile([P, PASSES, R], U16, name="wu_w", align_bytes=64)
        wu_s = [keep.tile([P, R], U8, name="wu_s%d" % a, align_bytes=64) for a in range(PASSES)]
        wd4_w = keep.tile([P, N // 2], I32, name="wd4_w", align_bytes=64)
        wd8_w = keep.tile([P, N], I32, name="wd8_w", align_bytes=64)
        wd_s = keep.tile([P, 2, N // 4], I32, name="wd_s", align_bytes=64)
        wg_raw = [keep.tile([P, PACK, PACK * (m1 - m0)], F32, name="wg_raw%d" % i, tag="wg_raw%d" % i, align_bytes=64) for i, (a, m0, m1) in enumerate(WG_PARTS)]
        wg_bf = [keep.tile([P, PACK, P, PACK], BF16, name="wg_bf%d" % a, tag="wg_bf%d" % a, align_bytes=64) for a in range(PASSES)]
        wg_w = keep.tile([P, PASSES, R], U32, name="wg_w", align_bytes=64)
        wg_s = keep.tile([P, PASSES, R], U8, name="wg_s", align_bytes=64)
        v_w = [keep.tile([P, PASSES, PIECE], U16, name="v_w%d" % g, align_bytes=64) for g in range(PIECES)]
        ub_first = [keep.tile([P, 2, PIECE, 2], F32, name="ub_first%d" % g, align_bytes=64) for g in range(2)]
        h_bf = keep.tile([P, J, PACK], BF16, name="h_bf", align_bytes=64)
        h_w = keep.tile([P, J], U32, name="h_w", align_bytes=64)
        h_s = keep.tile([P, J], U8, name="h_s", align_bytes=64)
        banks = [psum.tile([P, HALF], F32, name="bank%d" % b) for b in range(8)]
        picked = {}

        def up_bank(c):
            return banks[(0, 1, 2, 3, 4, 5, 0, 1)[c]]

        def gate_bank(c):
            return banks[(6, 7, 0, 1, 2, 3, 6, 7)[c]]

        def scale_rows(tile_rows, scales, r):
            nc.sync.dma_start(out=tile_rows, in_=scales.bitcast(I32)[:, r:16:4, :].rearrange("a q w -> q a w"))

        def load_wg(i):
            a, m0, m1 = WG_PARTS[i]
            rows = wg[a * K_PASS : (a + 1) * K_PASS, PACK * m0 : PACK * m1]
            nc.sync.dma_start(out=wg_raw[i][:], in_=rows.rearrange("(p i) r -> p i r", i=PACK))

        def gather_scales(s, tile):
            j0, j1 = SPANS[s]
            picked[s] = tile
            nc.vector.tensor_copy(out=picked[s][:].bitcast(U8), in_=tab_s[:].bitcast(U8).indirect(offsets[:, j0 // 16 : j1 // 16]))

        def shift(s):
            for p0, p1 in (((0, P - SHIFT),), ((0, 64), (64, 96), (96, 100)))[s]:
                nc.sync.dma_start(out=moved[s][p0:p1, :], in_=picked[s][p0 + SHIFT : p1 + SHIFT, :])

        def table_scale(a, j0, j1):
            s = j0 // HALF
            plane = picked[s] if a == 0 else moved[s]
            return plane[:].bitcast(U8)[:, j0 - SPANS[s][0] : j1 - SPANS[s][0]]

        def gather_words(g, got, count=1):
            listed = offsets[:, g * PIECE // 16 : (g + count) * PIECE // 16]
            nc.vector.tensor_copy(out=got[:], in_=tab_w[:].bitcast(U32).indirect(listed))
            return got[:]

        def part(g, got):
            nc.vector.tensor_copy(
                out=v_w[g][:].rearrange("p a (h j) -> p h a j", h=2),
                in_=got.bitcast(U16).rearrange("p (h j a) -> p h a j", h=2, a=PASSES),
            )

        def kept_plane(s):
            return keep.tile([P, (SPANS[s][1] - SPANS[s][0]) // 4], I32, name="picked%d" % s, align_bytes=64)

        def lane_tile(name, dtype, columns, offset):
            return lane.tile([P, columns], dtype, name=name, offset=offset, align_bytes=64)

        def first_layer(bank, c, a, weight, weight_scale, first):
            g, lo = divmod(c * CHUNK, PIECE)
            for t in range(PACK):
                nc.tensor.matmul_mx(
                    out=bank[:, t * CHUNK : (t + 1) * CHUNK],
                    lhsT=weight[:, a, t * P : (t + 1) * P],
                    lhsT_scale=weight_scale[:, t * P : (t + 1) * P],
                    rhs=v_w[g][:, a, lo : lo + CHUNK].bitcast(FP4X4),
                    rhs_scale=table_scale(a, c * CHUNK, (c + 1) * CHUNK),
                    start=(a == first and t == 0),
                    stop=(a != first and t == PACK - 1),
                )

        def up(c, a):
            first_layer(up_bank(c), c, a, wu_w[:].bitcast(FP4X4), wu_s[a], 1)

        def up_piece(g, a):
            for t in range(PACK):
                nc.tensor.matmul_mx(
                    out=banks[2 * g + t // 2][:, t % 2 * PIECE : (t % 2 + 1) * PIECE],
                    lhsT=wu_w[:].bitcast(FP4X4)[:, a, t * P : (t + 1) * P],
                    lhsT_scale=wu_s[a][:, t * P : (t + 1) * P],
                    rhs=v_w[g][:, a, :].bitcast(FP4X4),
                    rhs_scale=table_scale(a, g * PIECE, (g + 1) * PIECE),
                    start=(a == g and t % 2 == 0),
                    stop=(a != g and t % 2 == 1),
                )

        def gate(c, a):
            first_layer(gate_bank(c), c, a, wg_w[:].bitcast(FP8X4), wg_s[:, a, :], 0 if c < 4 else 1)

        gated = {}

        def activate(c):
            gated[c] = ring.tile([P, CHUNK, PACK], F32, name="gated")
            nc.scalar.activation(gated[c][:], gate_bank(c)[:].rearrange("p (t j) -> p j t", t=PACK), TANH)

        def multiply(c):
            rows = h_bf[:, c * CHUNK : (c + 1) * CHUNK, :]
            if c < 4:
                nc.vector.tensor_tensor(
                    rows.rearrange("p j (u e) -> p j u e", u=2),
                    ub_first[c // 2][:, :, c % 2 * CHUNK : (c % 2 + 1) * CHUNK, :].rearrange("p u j e -> p j u e"),
                    gated[c][:].rearrange("p j (u e) -> p j u e", u=2),
                    MULT,
                )
            else:
                nc.vector.tensor_tensor(rows, up_bank(c)[:].rearrange("p (t j) -> p j t", t=PACK), gated[c][:], MULT)

        def quantise_h(c0, c1):
            cols = slice(c0 * CHUNK, c1 * CHUNK)
            nc.vector.quantize_mx(
                out=h_w[:, cols].bitcast(FP8X4), scales=h_s[:, cols], in_=h_bf[:, cols, :].rearrange("p j t -> p (j t)")
            )

        def round_wg(copy, i, lo, hi):
            a, m0, m1 = WG_PARTS[i]
            copy(
                out=wg_bf[a][:, :, lo:hi, :].rearrange("p t m i -> p m i t"),
                in_=wg_raw[i][:, :, PACK * (lo - m0) : PACK * (hi - m0)].rearrange("p i (m t) -> p m i t", t=PACK),
            )

        def round_on_scalar(i):
            a, m0, m1 = WG_PARTS[i]
            if SCALAR_COLUMNS[i] > 0:
                round_wg(nc.scalar.copy, i, m0, m0 + SCALAR_COLUMNS[i])

        def round_on_vector(i):
            a, m0, m1 = WG_PARTS[i]
            if m0 + SCALAR_COLUMNS[i] < m1:
                round_wg(nc.vector.tensor_copy, i, m0 + SCALAR_COLUMNS[i], m1)

        def quantise_wg(a, t0, t1):
            cols = slice(t0 * P, t1 * P)
            nc.vector.quantize_mx(
                out=wg_w[:, a, cols].bitcast(FP8X4),
                scales=wg_s[:, a, cols],
                in_=wg_bf[a][:, t0:t1, :, :].rearrange("p t m i -> p (t m i)"),
            )

        def down(b, half, copy, bank):
            tiers = (
                wd4_w[:].bitcast(U16)[:, b * P : (b + 1) * P].bitcast(FP4X4),
                wd8_w[:, b * P : (b + 1) * P].bitcast(FP8X4),
            )
            cols = slice(half * HALF, (half + 1) * HALF)
            for tier in range(2):
                nc.tensor.matmul_mx(
                    out=bank[:],
                    lhsT=tiers[tier],
                    lhsT_scale=wd_s[:, tier, :].bitcast(U8)[:, b * P : (b + 1) * P],
                    rhs=h_w[:, cols].bitcast(FP8X4),
                    rhs_scale=h_s[:, cols],
                    start=(tier == 0),
                    stop=(tier == 1),
                )
            y = keep.tile([P, HALF], F32, name="y%d_%d" % (b, half))
            copy(out=y[:], in_=bank[:])
            nc.sync.dma_start(out=out[b * P : (b + 1) * P, cols], in_=y[:])

        for plane in (tab_s, wu_s_raw, moved[0], moved[1], wd_s):
            nc.vector.memset(plane[:], 0)

        nc.sync.dma_start(offsets[:], offs)
        nc.sync.dma_start(out=wu_w_raw[:], in_=wu_words.bitcast(I32).rearrange("a p w -> p a w"))
        for r in range(4):
            scale_rows(tab_s[r:P:SHIFT, :], tab_scales, r)
        nc.sync.dma_start(out=tab_w[:], in_=tab_words[0].rearrange("p t b -> p (t b)").bitcast(I32))
        for r in range(4):
            scale_rows(wu_s_raw[r:P:32, :, :], wu_scales, r)
        load_wg(0)
        gather_scales(0, kept_plane(0))
        shift(0)
        load_wg(1)
        gather_scales(1, kept_plane(1))
        shift(1)
        for i in range(WARM_UPS):
            nc.tensor.matmul_mx(
                out=banks[7][:],
                lhsT=wu_w_raw[:, 0, :].bitcast(U16)[:, 0:P].bitcast(FP4X4),
                lhsT_scale=picked[0][:].bitcast(U8)[:, 0:P],
                rhs=wu_w_raw[:, 1, :].bitcast(U16).bitcast(FP4X4),
                rhs_scale=tab_s[:].bitcast(U8)[:, 0:HALF],
                start=True,
                stop=True,
            )
        load_wg(2)
        load_wg(3)
        load_wg(4)

        part(0, gather_words(0, lane_tile("got0", U32, PIECE, 0)))
        for a in range(PASSES):
            nc.gpsimd.tensor_copy(
                out=wu_s[a][:].rearrange("p (t m) -> p t m", t=PACK),
                in_=wu_s_raw[:, a, :].bitcast(U8).rearrange("p (m t) -> p t m", t=PACK),
            )
        nc.vector.tensor_copy(
            out=wu_w[:].rearrange("p a (t m) -> p a t m", t=PACK),
            in_=wu_w_raw[:].bitcast(U16).rearrange("p a (m t) -> p a t m", t=PACK),
        )
        part(1, gather_words(1, lane_tile("got1", U32, PIECE, 0)))
        part(2, gather_words(2, lane_tile("got2", U32, PIECE, 0)))
        for g in range(2):
            up_piece(g, g)
            up_piece(g, 1 - g)
        for c in (4, 5):
            up(c, 1)
            up(c, 0)
        nc.sync.dma_start(out=wd4_w[:], in_=wd4_words[0].bitcast(I32))
        nc.sync.dma_start(out=wd8_w[:], in_=wd8_words[0].rearrange("p n b -> p (n b)").bitcast(I32))
        for tier, scales in enumerate((wd4_scales, wd8_scales)):
            for r in range(4):
                scale_rows(wd_s[r:P:32, tier : tier + 1, :], scales, r)

        round_on_scalar(0)
        round_on_scalar(1)
        round_on_scalar(2)
        for b in range(4):
            nc.scalar.copy(out=ub_first[b // 2][:, b % 2, :, :], in_=banks[b][:].rearrange("p (e j) -> p j e", e=2))
        quantise_wg(0, 0, 4)
        for c in range(4):
            gate(c, 0)
        round_on_vector(3)
        round_on_vector(4)
        quantise_wg(1, 0, 4)
        part(3, gather_words(3, keep.tile([P, PIECE], U32, name="got3", tag="wg_bf1", align_bytes=64)))

        for c in range(4):
            gate(c, 1)
        for c in (4, 5):
            gate(c, 1)
            gate(c, 0)
        for c in range(CHUNKS):
            activate(c)
            if c < 2:
                gate(c + 6, 1)
                gate(c + 6, 0)
            elif c < 4:
                up(c + 4, 1)
                up(c + 4, 0)
            if c == CHUNKS - 1:
                down(0, 0, nc.scalar.copy, banks[2])
            multiply(c)
            if c in (2, 4):
                quantise_h(c - 2, c)
            if c == 6:
                quantise_h(4, 6)
            if c == 7:
                quantise_h(6, 7)
        quantise_h(7, 8)
        copies = (nc.scalar.copy, nc.vector.tensor_copy)
        for i in range(1, 8):
            half, b = divmod(i, 4)
            down(b, half, copies[half and b % 2], banks[(2, 3, 6, 7, 4, 5, 0, 1)[i]])
